import numpy as np, ml_dtypes
CORES = [3,11,19,27,35,43,51,59]
N = 8
BF = ml_dtypes.bfloat16
W, L, OR, ST, NEED = 4096, 128, 16, 2, 10
def forest(rng):
    o = np.argsort(rng.random((N, 8, 16, L, OR)), axis=2); k = np.arange(16).reshape(1, 1, 16, 1, 1)
    q = (rng.random(o.shape) * k).astype(np.int64); p = np.zeros_like(o)
    np.put_along_axis(p, o, np.take_along_axis(o, q, 2), 2)
    return np.where(rng.random(p.shape) < 0.1, k, p)
def limits(rng, lo, n):
    base = np.argsort(rng.random((N, 8, 1, L)), axis=-1) % n + lo
    return np.clip(base + rng.integers(-2, 3, (N, 8, 16, L)), 0, 15)
def parts(rng):
    x = rng.integers(0, 16, (N, 8, 16, W)); c = rng.integers(0, W, (N, 8, 16, L, OR)); p = forest(rng); a = limits(rng, 3, 8)
    v = rng.integers(0, 33, (N, 8, OR, L))
    o = np.arange(OR).reshape(1, 1, OR, 1); fav = rng.integers(0, OR, (1, 8, 1, L)); stick = rng.random((1, 8, 1, L)) < 0.5
    v = np.where(stick, np.where(o == fav, rng.integers(20, 33, v.shape), rng.integers(0, 7, v.shape)), v)
    return x, c, p, a, v
def bf(a): return np.ascontiguousarray(a).astype(np.float32).astype(BF)
def pack(x, c, p, a, v):
    return {"xt": bf(x.reshape(N, 128, W)), "pg": np.ascontiguousarray(c.reshape(N, 128, L * OR)).astype(np.int32), "pre": bf(p.reshape(N, 128, L * OR)),
            "lim": bf(a.reshape(N, 128, L)), "vv": np.ascontiguousarray(v.reshape(N, 8 * OR, L)).astype(np.int32)}
def setup_inputs(rng):
    return pack(*parts(rng))
def setup_inputs_ties(rng):
    x, c, p, a, v = parts(rng)
    dl = rng.integers(1, 8, (1, 8, 1, 1)); x = rng.integers(0, 9, (N, 8, 16, 1)) + dl * rng.integers(0, 2, x.shape)
    k = np.argsort(rng.random((N, 8, 1, L)), axis=-1) % 5; n = np.array([0, 2 * NEED - 16, 2 * NEED - 15, NEED - 1, 16])[k]
    a = np.where(np.argsort(rng.random(a.shape), axis=2) < n, dl, dl - 1)
    t = rng.choice(np.array([0, 1, 16, 31, 32]), (N, 8, 1, L))
    v = np.where(np.argsort(rng.random(v.shape), axis=2) < 2, t, np.minimum(rng.integers(0, 33, v.shape), t))
    return pack(x, c, p, a, v)
def setup_inputs_ends(rng):
    x, c, p, a, v = parts(rng)
    x = 15 * rng.integers(0, 2, x.shape); x[..., 0] = 0; x[..., W - 1] = 15
    e = rng.choice(np.array([0, 1, W // 2, W - 2, W - 1]), c.shape); c = np.where(rng.random((N, 8, 1, L, 1)) < 0.5, e, c)
    T = np.arange(16).reshape(1, 1, 16, 1, 1); k = rng.integers(0, 6, (N, 8, 1, L, 1))
    q = np.where(k == 0, T, np.where(k == 1, np.maximum(T - 1, 0), np.where(k == 2, 0, np.where(k == 3, 15, (T + 1) % 16))))
    p = np.where(k == 5, rng.integers(0, 16, p.shape), q)
    k = np.argsort(rng.random((N, 8, 1, L)), axis=-1) % 5; pos = np.argsort(rng.random(a.shape), axis=2)
    a = np.where(k == 0, 0, np.where(k == 1, 15, np.where(k == 2, 14, np.where(pos < np.where(k == 3, NEED, NEED - 1), 15, 0))))
    o = np.arange(OR).reshape(1, 1, OR, 1); k = rng.integers(0, 5, (N, 8, 1, L))
    v = np.where(k == 0, 0, np.where(k == 1, 32, np.where(k == 2, 32 * (o == 0), np.where(k == 3, 32 * (o == OR - 1), v))))
    z = int(rng.integers(0, 8)); w = np.argsort(rng.random(L)) % 4; x[:, z] = 15 * (np.arange(W) & 1)
    tt = T[0]; ring = (w == 0).reshape(1, 1, L, 1); climb = (w == 1).reshape(1, 1, L, 1)
    par = rng.integers(0, 2, (N, 1, L, OR)); even = c[:, z] - (c[:, z] & 1)
    c[:, z] = np.where(ring, even + ((par + tt) & 1), np.where(climb, even + ((par + (tt == 15)) & 1), c[:, z]))
    p[:, z] = np.where(ring, (tt + 1) % 16, np.where(climb, 0, p[:, z]))
    a = np.where(w == 1, 15, a); a[:, z] = np.where(w <= 1, 14 * rng.integers(0, 2, (N, 16, L)), a[:, z])
    v[:, z] = np.where(w == 1, 32 * (o[0] < 5) - 1 * (o[0] == 3), v[:, z])
    return pack(x, c, p, a, v)
def setup_inputs_alike(rng):
    x, c, p, a, v = parts(rng)
    x[:, ::2] = x[:, ::2][..., rng.integers(0, 8, W)]
    few = rng.integers(0, W, 5); few[0] = 0; few[1] = W - 1; c = few[rng.integers(0, 5, c.shape)]
    m = (rng.random((N, 8, 1, L, 1)) < 0.3) | (rng.random((N, 1, 1, L, 1)) < 0.3)
    c = np.where(m, c[:, :, :1], c); a[:, rng.integers(0, 8)] = 0
    return pack(x, c, p, a, v)
def setup_inputs_same(rng):
    x, c, p, a, v = parts(rng)
    o = np.arange(OR).reshape(1, 1, OR, 1); fav = rng.integers(0, OR, (1, 8, 1, L))
    v = np.where(o == fav, 32, rng.integers(0, 3, v.shape)); a = limits(rng, 5, 6)
    a[:, rng.integers(0, 8)] = rng.integers(0, 5, (N, 16, L))
    return pack(x, c, p, a, v)
def setup_inputs_spread(rng):
    x, c, p, a, v = parts(rng); E = np.array([0.25, 0.5, 1.0, 2.0, 4.0])
    def un(n, shape, by): return np.minimum((n * rng.random(shape) ** rng.choice(E, by)).astype(np.int64), n - 1)
    x = un(16, x.shape, (N, 8, 16, 1)); c = un(W, c.shape, (N, 8, 1, L, OR)); a = un(16, a.shape, (N, 8, 1, L)); v = un(33, v.shape, (N, 8, OR, 1))
    return pack(x, c, p, a, v)
def check_inputs(d):
    bad = []
    for k, hi in (("xt", 15), ("pg", W - 1), ("pre", 15), ("lim", 15), ("vv", 32)):
        b = np.asarray(d[k]).astype(np.float64)
        if not (np.min(b) >= 0 and np.max(b) <= hi and np.all(b == np.floor(b))): bad.append("range of " + k)
    return bad
def reference(xt, pg, pre, lim, vv):
    xs = np.ascontiguousarray(xt.astype(np.int32).reshape(N, 8, 16, W).transpose(0, 1, 3, 2))
    cur = np.ascontiguousarray(pg.astype(np.int64).reshape(N, 8, 16, L, OR).transpose(0, 1, 3, 4, 2))
    prd = np.ascontiguousarray(pre.astype(np.int64).reshape(N, 8, 16, L, OR).transpose(0, 1, 3, 4, 2))
    a = np.ascontiguousarray(lim.astype(np.int32).reshape(N, 8, 16, L).transpose(0, 1, 3, 2))
    v = np.ascontiguousarray(vv.astype(np.int64).reshape(N, 8, OR, L).transpose(0, 1, 3, 2))
    m = np.zeros((N, 8, L), np.int64)
    g0 = np.arange(8).reshape(1, 8, 1); l0 = np.arange(L).reshape(1, 1, L)
    for s in range(N):
        h = ((np.arange(N) + s) % N).reshape(N, 1, 1)
        o = np.argmax(v, axis=3)
        c = cur[h, g0, l0, o]; p = prd[h, g0, l0, o]
        got = np.zeros((N, 8, L), np.int64)
        for t in range(ST):
            F = xs[h[..., None], g0[..., None], c]
            G = np.take_along_axis(F, p[..., None], 3)
            D = np.abs(F - G)
            ok = np.add.reduce((D <= a[:, :, :, None, :]).astype(np.int64), axis=4) >= NEED
            full = np.all(ok, axis=3)
            got = got + full
            c = np.where(full[..., None], (5 * c + 1) & (W - 1), np.where(ok, c, (5 * c + np.add.reduce(D, axis=4) + 1) & (W - 1)))
        cur[h, g0, l0, o] = c
        m = m + got
        odd = np.add.reduce(got, axis=1, keepdims=True) & 1
        v = v + 1 + odd[..., None]
        np.put_along_axis(v, o[..., None], np.add.reduce(ok.astype(np.int64), axis=3)[..., None], 3)
    return {"yg": np.ascontiguousarray(cur.transpose(0, 1, 4, 2, 3)).reshape(N, 128, L * OR).astype(np.float32),
            "yv": np.ascontiguousarray(v.transpose(0, 1, 3, 2)).reshape(N, 8 * OR, L).astype(np.float32), "ym": m.astype(np.float32)}

@@ -1,0 +1,410 @@
+from concourse.bass import DstId, RemoteDMATransfer
+from concourse.mybir import AluOpType as ALU, AxisListType, ActivationFunctionType as AF
+
+N, NB, LB, NS = 8, 2, 64, 4
+LS = LB // NS
+CB, CS = 16 * LB, 16 * LS
+MW = 80
+GS = ((1, 3),)
+BON, LOOK = 3.0, 0.1
+KB = 1 << 19
+W15 = 1 << 15
+THR = 10 * W15
+
+SCRATCH = {
+    "xw": ("sbuf", [128, 4096], "bfloat16"), "pw": ("sbuf", [128, 2048], "bfloat16"),
+    "pgi": ("sbuf", [128, 2048], "int32"), "cw": ("sbuf", [128, 2048], "float32"),
+    "vt": ("sbuf", [128, 128], "int32"), "vtb": ("sbuf", [128, 128], "bfloat16"),
+    "limo": ("sbuf", [128, 128], "bfloat16"), "limt": ("sbuf", [128, 128 * N], "bfloat16"),
+    "minb": ("sbuf", [128, MW * NB * (N + 1)], "float32"), "mout": ("sbuf", [128, MW * NB * N], "float32"),
+    "mia": ("sbuf", [128, 8 * NB * N], "int32"), "mxo": ("sbuf", [128, 8 * NB * N], "int32"),
+    "onef": ("sbuf", [128, 128], "float32"), "oneb": ("sbuf", [128, 128], "bfloat16"), "posb": ("sbuf", [128, 128], "bfloat16"),
+    "bias": ("sbuf", [128, 1], "float32"),
+    "idf": ("sbuf", [128, 128], "float32"), "idb": ("sbuf", [128, 128], "bfloat16"), "nid": ("sbuf", [128, 128], "bfloat16"),
+    "idp": ("sbuf", [128, 128], "float32"), "idn": ("sbuf", [128, 128], "float32"),
+    "bo0": ("sbuf", [128, 128], "bfloat16"), "bo": ("sbuf", [128, 128], "bfloat16"),
+    "bq1": ("sbuf", [128, 128], "float32"), "bq2": ("sbuf", [128, 128], "float32"), "bq": ("sbuf", [128, 128], "bfloat16"),
+    "pmt": ("sbuf", [128, 128], "bfloat16"), "es": ("sbuf", [128, 2048], "bfloat16"), "ew": ("sbuf", [128, 2048], "bfloat16"),
+    "ex": ("sbuf", [128, 2048], "bfloat16"),
+    "ix": ("sbuf", [128, 128], "int32"), "ix2": ("sbuf", [128, 128], "int32"), "ml": ("sbuf", [128, 128], "bfloat16"),
+    "ka": ("sbuf", [128, 64], "int32"), "ka2": ("sbuf", [128, 64], "int32"), "kb": ("sbuf", [128, 64], "int32"), "ck": ("sbuf", [128, 64], "float32"),
+    "ckd": ("sbuf", [128, 4], "float32"), "r16": ("sbuf", [128, 64], "bfloat16"),
+    "cli": ("sbuf", [128, 4], "int32"), "cli2": ("sbuf", [128, 4], "int32"), "cl": ("sbuf", [128, 4], "uint16"),
+    "e4a": ("sbuf", [128, 64], "bfloat16"), "e4": ("sbuf", [128, 64], "bfloat16"), "e4s": ("sbuf", [128, 64], "bfloat16"), "e4n": ("sbuf", [128, 64], "bfloat16"),
+}
+for _b in range(NB):
+    for _n, _c, _d in (("f", CB, "bfloat16"), ("gq", CB, "bfloat16"), ("a", CB, "bfloat16"), ("m", CB, "bfloat16"),
+                       ("li", 4, "int32"), ("ls", 4, "uint16"), ("cf", 64, "float32"), ("co", 64, "uint16"),
+                       ("lk", 4, "float32"), ("mo", 4, "float32"), ("nk", 4, "float32"),
+                       ("pg_", 64, "bfloat16"), ("po", 64, "uint16"), ("a5", 64, "float32"), ("ax", 64, "float32"),
+                       ("pa", 64, "bfloat16"), ("bm", 64, "float32"), ("yi", 64, "int32"), ("ci", 64, "int32"),
+                       ("f8", 16, "bfloat16"), ("mm", 4, "float32"), ("mn", 4, "int32"), ("od", 4, "int32"), ("rb", 64, "bfloat16"),
+                       ("mk", 128, "bfloat16"), ("ns", 64, "float32"), ("se", 64, "float32"), ("ua", 64, "float32"),
+                       ("vo", 128, "float32"), ("yo", 64, "float32")):
+        SCRATCH["%s%d" % (_n, _b)] = ("sbuf", [128, _c], _d)
+for _b in range(8):
+    SCRATCH["pb%d" % _b] = ("psum", [128, 512], "float32")
+
+SEMAPHORES = ["qv", "qs", "qt", "qg", "lsem", "limr", "dlim", "dvv", "dxt"]
+SEMAPHORES += ["%s%d" % (n, b) for n in ("dpg", "dpre", "oyg", "oyv", "oym") for b in range(NB)]
+SEMAPHORES += ["h%d_%d" % (s, b) for s in range(1, N + 1) for b in range(NB)] + ["k%d_%d" % (s, b) for s in range(1, N) for b in range(NB)]
+
+CYC, FAC, WAKE, XG, PEC, HOP = 0.00083, 1.25, 0.1, 1.56, 0.0005, 2.0
+
+
+def cv(n):
+    return max(64, n) * CYC * FAC
+
+
+def cg(n):
+    return (0.055 + XG * n * CYC) * FAC
+
+
+def ct(n):
+    return n * PEC
+
+
+def schedule(nodes):
+    n = len(nodes)
+    succ = [[] for _ in range(n)]
+    for i, d in enumerate(nodes):
+        for j in d["dep"]:
+            succ[j].append(i)
+    pri = [0.0] * n
+    for i in range(n - 1, -1, -1):
+        d = nodes[i]
+        pri[i] = d["c"] + d["lat"] + WAKE + max([pri[k] for k in succ[i]] + [0.0])
+    for i in range(n):
+        pri[i] -= nodes[i]["bl"]
+    left = [len(d["dep"]) for d in nodes]
+    ready = [0.0] * n
+    free = {"v": 0.0, "s": 0.0, "t": 0.0, "g": 0.0, "y": 0.0}
+    pool = {q: [] for q in list(free) + ["r"]}
+    for i in range(n):
+        if left[i] == 0:
+            pool[nodes[i]["q"]].append(i)
+    order = []
+    while len(order) < n:
+        best = None
+        for q in pool:
+            if not pool[q]:
+                continue
+            f = free.get(q, 0.0)
+            t0 = min(max(f, ready[i]) for i in pool[q])
+            i = max((i for i in pool[q] if max(f, ready[i]) <= t0 + LOOK), key=lambda i: pri[i])
+            st = max(f, ready[i])
+            if best is None or st < best[0]:
+                best = (st, q, i)
+        st, q, i = best
+        pool[q].remove(i)
+        en = st + nodes[i]["c"]
+        if q != "r":
+            free[q] = en
+        order.append(i)
+        for k in succ[i]:
+            w = 0.0 if (nodes[k]["q"] == q and not nodes[k]["dep"][i]) else WAKE
+            ready[k] = max(ready[k], en + nodes[i]["lat"] + w)
+            left[k] -= 1
+            if left[k] == 0:
+                pool[nodes[k]["q"]].append(k)
+    return order
+
+
+def rank_program(g, core, T, topo):
+    rank = T.rank_of(core)
+    if rank is None:
+        return
+    eng = {"v": g.vector, "s": g.scalar, "t": g.tensor, "g": g, "y": g.sync}
+    csem = {"v": "qv", "s": "qs", "t": "qt", "g": "qg"}
+    nodes, last, cur = [], {}, [0.0]
+
+    def add(q, fns, R=(), W=(), c=0.08, sem=None, val=None, after=(), lat=0.0):
+        i = len(nodes)
+        dep = {}
+        for (acc, wr) in ((R, False), (W, True)):
+            for (buf, a, b) in acc:
+                bank = buf[:2] == "pb"
+                rec = last.setdefault(buf, [])
+                for (j, ja, jb, jw) in rec:
+                    if j == i or (not bank and (ja >= b or jb <= a)):
+                        continue
+                    same = nodes[j]["q"] == q
+                    if not (wr or jw) and (same or not bank):
+                        continue
+                    need = not (same and (q == "t" or not jw))
+                    dep[j] = dep.get(j, False) or need
+                if wr:
+                    if bank and q == "t":
+                        rec[:] = [r for r in rec if r[0] == i]
+                    elif not bank:
+                        rec[:] = [r for r in rec if r[0] == i or not (r[1] >= a and r[2] <= b)]
+                rec.append((i, a, b, wr))
+        for j in after:
+            dep[j] = dep.get(j, False)
+        nodes.append({"q": q, "f": fns if isinstance(fns, list) else [fns], "dep": dep, "c": c, "sem": sem, "val": val, "lat": lat, "bl": cur[0]})
+        return i
+
+    t = T
+    nm = lambda n, b: "%s%d" % (n, b)
+    v, sc, te = g.vector, g.scalar, g.tensor
+    IDF, CK, IDB, NID, BO = ("idf", 0, 128), ("ck", 0, 64), ("idb", 0, 128), ("nid", 0, 128), ("bo", 0, 128)
+
+    def load(fns, W, sem, cost, q="y"):
+        add(q, fns, (), W, 0.06 * len(fns), sem, 16 * len(fns), (), cost)
+    load([lambda k=k: g.scalar.dma_start(t.vt[:, 16 * k:16 * k + 16], t.vv[16 * k:16 * k + 16, :]) for k in range(8)], [("vt", 0, 128)], "dvv", 3.0, "s")
+    for b in range(NB):
+        load([lambda b=b: g.sync.dma_start(t.pgi[:, CB * b:CB * b + CB], t.pg[:, CB * b:CB * b + CB])], [("pgi", CB * b, CB * b + CB)], nm("dpg", b), 4.0 + 4 * b)
+        if b == 0:
+            load([lambda: g.sync.dma_start(t.xw[:], t.xt[:])], [("xw", 0, 4096)], "dxt", 6.5)
+        load([lambda b=b: g.sync.dma_start(t.pw[:, CB * b:CB * b + CB], t.pre[:, CB * b:CB * b + CB])], [("pw", CB * b, CB * b + CB)], nm("dpre", b), 7.0 + 2 * b)
+        if b == 0:
+            load([lambda: g.sync.dma_start(t.limo[:], t.lim[:])], [("limo", 0, 128)], "dlim", 7.5)
+
+    def vmem(buf, a, b, val):
+        add("v", lambda: v.memset(t[buf][:, a:b], val), (), [(buf, a, b)], cv((b - a) * (0.5 if SCRATCH[buf][2] == "bfloat16" else 1)))
+
+    def vts(out, in0, n, fn, half=False):
+        add("v", fn, [(in0, 0, n)], [(out, 0, n)], cv(n * (0.5 if half else 1)))
+
+    def gen(out, n, fn, in_=None):
+        add("g", fn, [(in_, 0, n)] if in_ else (), [(out, 0, n)], (0.17 + 2 * n * CYC) * FAC)
+    vmem("onef", 0, 128, 1.0)
+    vmem("oneb", 0, 128, 1.0)
+    vmem("posb", 0, 128, 1024.0)
+    vmem("bias", 0, 1, -15.0)
+    gen("idf", 128, lambda: g.affine_select(t.idf[:], t.onef[:], [[-1, 128]], ALU.is_equal, 0.0, 0, 1), "onef")
+    gen("pmt", 128, lambda: g.affine_select(t.pmt[:], t.posb[:], [[-4, 2], [-8, 16], [-1, 4]], ALU.is_equal, 0.0, 0, 1), "posb")
+    gen("ka", 64, lambda: g.iota(t.ka[:], [[0, 64]], 0, 16))
+    gen("kb", 64, lambda: g.iota(t.kb[:], [[-1, 16], [-256, 4]], 65536 + 1023, 0))
+    gen("cli", 4, lambda: g.iota(t.cli[:], [[0, 4]], 0, 1))
+    gen("r16", 64, lambda: g.iota(t.r16[:], [[0, NS], [16, LS]], 0, 0, allow_small_or_imprecise_dtypes=True))
+    gen("bo0", 128, lambda: g.affine_select(t.bo0[:], t.oneb[:], [[-16, 8], [0, 16]], ALU.is_ge, 0.0, 0, 1), "oneb")
+    gen("bo", 128, lambda: g.affine_select(t.bo[:], t.bo0[:], [[16, 8], [0, 16]], ALU.is_ge, 0.0, 15, -1), "bo0")
+    gen("es", 2048, lambda: g.iota(t.es[:], [[0, 2048]], 0, 0, allow_small_or_imprecise_dtypes=True))
+    gen("ix", 128, lambda: g.iota(t.ix[:], [[-1, 128]], 128, 1))
+    gen("e4a", 64, lambda: g.affine_select(t.e4a[:], t.oneb[:, 0:64], [[0, 16], [-16, 4]], ALU.is_ge, 0.0, 0, 1), "oneb")
+    gen("e4", 64, lambda: g.affine_select(t.e4[:], t.e4a[:], [[0, 16], [16, 4]], ALU.is_ge, 0.0, 15, -1), "e4a")
+    gen("mout", MW * NB * N, lambda: g.iota(t.mout[:], [[0, MW * NB * N]], 0, 0, allow_small_or_imprecise_dtypes=True))
+    vts("idb", "idf", 128, lambda: v.tensor_copy(t.idb[:], t.idf[:]))
+    add("v", lambda: v.tensor_copy(t.vtb[:], t.vt[:]), [("vt", 0, 128)], [("vtb", 0, 128)], cv(128))
+    vts("ka2", "ka", 64, lambda: v.tensor_scalar(t.ka2[:], t.ka[:], 255, None, ALU.bitwise_and))
+    add("v", lambda: v.tensor_tensor(t.ck[:], t.kb[:], t.ka2[:], ALU.subtract), [("ka2", 0, 64), ("kb", 0, 64)], [CK], cv(128))
+    vts("cli2", "cli", 4, lambda: v.tensor_scalar(t.cli2[:], t.cli[:], 3, None, ALU.bitwise_and))
+    vts("cl", "cli2", 4, lambda: v.tensor_copy(t.cl[:], t.cli2[:]))
+    add("v", lambda: v.tensor_scalar(t.ckd[:], t.ck[:, 0:4], -1.0, 65536.0, ALU.mult, ALU.add), [CK], [("ckd", 0, 4)], cv(4))
+    for b in range(NB):
+        add("v", lambda b=b: v.tensor_copy(t.cw[:, CB * b:CB * b + CB], t.pgi[:, CB * b:CB * b + CB]), [("pgi", CB * b, CB * b + CB)], [("cw", CB * b, CB * b + CB)], cv(CB))
+
+    def mi(s, b):
+        return MW * (NB * s + b)
+    for b in range(NB):
+        o = mi(0, b)
+        pb = nm("pb", 6 + b)
+        add("t", [lambda b=b, pb=pb: te.matmul(t[pb][:, 448:512], t.vtb[:], t.pmt[:, 64 * b:64 * b + 64], True, True)],
+            [("vtb", 0, 128), ("pmt", 0, 128)], [(pb, 0, 512)], ct(64))
+        add("v", lambda o=o, pb=pb: v.tensor_tensor(t.minb[:, o:o + 64], t.ck[:], t[pb][:, 448:512], ALU.add), [(pb, 0, 512), CK], [("minb", o, o + 64)], cv(64))
+        vmem("minb", o + 64, o + 80, 0.0)
+        for j in range(4):
+            add("v", lambda j=j, b=b, o=o: v.tensor_reduce(t.mia[:, 8 * b + j:8 * b + j + 1], t.minb[:, o + j:o + 64:4], AxisListType.X, ALU.max),
+                [("minb", o, o + 64)], [("mia", 8 * b + j, 8 * b + j + 1)], cv(16))
+    add("t", lambda: te.matmul(t.pb4[:, 0:128], t.limo[:], t.idb[:], True, True), [("limo", 0, 128), IDB], [("pb4", 0, 512)], ct(128))
+    add("s", lambda: sc.activation(t.limt[:, 0:128], t.pb4[:, 0:128], AF.Copy), [("pb4", 0, 512)], [("limt", 0, 128)], cv(128))
+    nxt = T.cores[(rank + 1) % N]
+    nrid, npid, _ = topo.addr(nxt)
+    nmask = topo.mask(core, nxt)
+    nne = bin(nmask).count("1")
+    dst, dsts, mask = [], [], nmask
+    for s in range(1, N):
+        d = T.cores[(rank + s) % N]
+        rid, pid, _ = topo.addr(d)
+        mask &= topo.mask(core, d)
+        dst.append(DstId(rid=rid, pnc=pid))
+        dsts.append(t.limt[:, 128 * s:128 * s + 128])
+    ne = bin(mask).count("1")
+    limsend = add("g", lambda: g.remote_dma_fused([RemoteDMATransfer(dst_ids=dst, dma_engine_mask=mask, remote_sem=t.sem.limr,
+                  srcs=[t.limt[:, 0:128]], dsts=dsts)], local_sem=t.sem.lsem), [("limt", 0, 128)], (), 2.0, "lsem", -ne)
+    add("r", [], (), [("limt", 128, 128 * N)], 4.0, "limr", 7 * ne, (limsend,))
+
+    for k in range(16):
+        add("s", lambda k=k: sc.activation(t.ex[:, k::16], t.idb[:], AF.Copy), [IDB], [("ex", 0, 2048)], cv(128))
+    for k in range(16):
+        add("v", lambda k=k: v.tensor_copy(t.es[:, 128 * k + k:128 * k + 128:16], t.bo[:, k::16]), [BO], [("es", 128 * k, 128 * k + 128)], cv(8))
+    add("v", lambda: v.tensor_scalar(t.ew[:], t.es[:], float(W15), None, ALU.mult), [("es", 0, 2048)], [("ew", 0, 2048)], cv(1024))
+    vts("bq1", "idb", 128, lambda: v.tensor_scalar(t.bq1[:], t.idb[:], float(-32 * KB), None, ALU.mult))
+    vts("bq2", "bo", 128, lambda: v.tensor_scalar(t.bq2[:], t.bo[:], float(KB), None, ALU.mult))
+    add("v", lambda: v.tensor_tensor(t.bq[:], t.bq1[:], t.bq2[:], ALU.add), [("bq1", 0, 128), ("bq2", 0, 128)], [("bq", 0, 128)], cv(256))
+    vts("nid", "idb", 128, lambda: v.tensor_scalar(t.nid[:], t.idb[:], -1.0, None, ALU.mult), True)
+    vts("ix2", "ix", 128, lambda: v.tensor_scalar(t.ix2[:], t.ix[:], 15, None, ALU.bitwise_and))
+    vts("ml", "ix2", 128, lambda: v.tensor_scalar(t.ml[:], t.ix2[:], 0.0, None, ALU.is_equal))
+    vts("e4s", "e4", 64, lambda: v.tensor_scalar(t.e4s[:], t.e4[:], -1024.0, None, ALU.mult), True)
+    vts("e4n", "e4", 64, lambda: v.tensor_scalar(t.e4n[:], t.e4[:], 1024.0, None, ALU.mult), True)
+    vts("idp", "idf", 128, lambda: v.tensor_scalar(t.idp[:], t.idf[:], 1.0 / 1024, None, ALU.mult))
+    vts("idn", "idf", 128, lambda: v.tensor_scalar(t.idn[:], t.idf[:], -1.0 / 1024, None, ALU.mult))
+
+    def slice_block(s, b):
+        o, q0 = mi(s, b), MW * (NB * s + b)
+        L = lambda n, a=0, e=64: (nm(n, b), a, e)
+        x = lambda n: t[nm(n, b)]
+        U, UR = t.minb[:, o:o + 64], ("minb", o, o + 64)
+        cs, ce = CB * b, CB * b + CB
+        LX, RB, QB = [nm("pb", 2 * b), nm("pb", 2 * b + 1)], nm("pb", 4 + b), nm("pb", 6 + b)
+        ALL = lambda bank: (bank, 0, 512)
+        k0 = 8 * (NB * s + b)
+        MI, MIR = t.mia[:, k0:k0 + 4], ("mia", k0, k0 + 4)
+        add("v", lambda: v.tensor_scalar(x("li")[:, 0:4], MI, 1023, None, ALU.bitwise_and), [MIR], [L("li", 0, 4)], cv(4))
+        add("v", lambda: v.tensor_scalar(x("ls")[:, 0:4], x("li")[:, 0:4], -1.0, 1023.0, ALU.mult, ALU.add), [L("li", 0, 4)], [L("ls", 0, 4)], cv(4))
+        add("s", lambda: sc.activation(x("cf")[:], t.cw[:, cs:ce].indirect(x("ls")[:, 0:4]), AF.Copy), [("cw", cs, ce), L("ls", 0, 4)], [L("cf")], cg(64))
+        add("v", lambda: v.tensor_copy(x("co")[:], x("cf")[:]), [L("cf")], [L("co")], cv(64))
+        add("s", lambda: sc.activation(x("pg_")[:], t.pw[:, cs:ce].indirect(x("ls")[:, 0:4]), AF.Copy), [("pw", cs, ce), L("ls", 0, 4)], [L("pg_")], cg(64))
+        add("t", [lambda: te.matmul(t[QB][:, 64:128], t.idb[:], x("pg_")[:], True, False), lambda: te.matmul(t[QB][:, 64:128], t.idb[:], t.r16[:], False, True)],
+            [IDB, L("pg_"), ("r16", 0, 64)], [ALL(QB)], ct(128))
+        add("v", lambda: v.tensor_copy(x("po")[:], t[QB][:, 64:128]), [ALL(QB)], [L("po")], cv(64))
+        for st in range(2):
+            if st == 0:
+                for h in range(2):
+                    add("t", lambda h=h: te.matmul(t[LX[h]][:], t.limt[:, 128 * s:128 * s + 128], t.ex[:, cs + 512 * h:cs + 512 * h + 512], True, True),
+                        [("limt", 128 * s, 128 * s + 128), ("ex", 0, 2048)], [ALL(LX[h])], ct(512))
+            else:
+                add("v", lambda: v.tensor_copy(x("cf")[:], x("ci")[:]), [L("ci")], [L("cf")], cv(64))
+
+            def piece(u):
+                p0, p1, l0, l1 = CS * u, CS * u + CS, LS * u, LS * u + LS
+                lb, c0, DB = LX[p0 // 512], p0 % 512, (QB, RB)[u % 2]
+                f, gq, a, m = [x(n)[:, p0:p1] for n in ("f", "gq", "a", "m")]
+                win = lambda: x("f")[:, p0:p1].indirect(x("po")[:, l0:l1])
+                add("s", lambda: sc.activation(f, t.xw[:].indirect(x("co")[:, l0:l1]), AF.Copy), [("xw", 0, 4096), L("co", l0, l1)], [L("f", p0, p1)], cg(CS))
+                gio = [L("f", p0, p1), L("po", l0, l1)], [L("gq", p0, p1)], cg(CS)
+                if (st, u) in GS:
+                    add("s", lambda: sc.activation(gq, win(), AF.Copy), *gio)
+                else:
+                    add("v", lambda: v.tensor_copy(gq, win()), *gio)
+                add("t", [lambda: te.matmul(t[DB][:, 192:192 + CS], t.idb[:], f, True, False), lambda: te.matmul(t[DB][:, 192:192 + CS], t.nid[:], gq, False, True)],
+                    [IDB, NID, L("f", p0, p1), L("gq", p0, p1)], [ALL(DB)], ct(2 * CS))
+                add("s", lambda: sc.activation(a, t[DB][:, 192:192 + CS], AF.Abs), [ALL(DB)], [L("a", p0, p1)], cv(CS))
+                add("v", lambda: v.tensor_tensor(m, a, t[lb][:, c0:c0 + CS], ALU.is_le), [L("a", p0, p1), ALL(lb)], [L("m", p0, p1)], cv(CS))
+            for u in range(NS):
+                piece(u)
+            add("s", lambda: sc.activation(x("a5")[:], x("cf")[:], AF.Copy, bias=float(1 - 17 * KB), scale=5.0), [L("cf")], [L("a5")], cv(64))
+            add("s", lambda: sc.activation(x("ax")[:], x("cf")[:], AF.Copy, bias=float(1 - 17 * KB + THR), scale=5.0), [L("cf")], [L("ax")], cv(64))
+            add("t", [lambda: te.matmul(t[RB][:, 0:64], t.idf[:], x("a5")[:], True, False)] +
+                [lambda k=k: te.matmul(t[RB][:, 0:64], t.es[:, 128 * k:128 * k + 128], x("a")[:, k::16], False, False) for k in range(16)],
+                [IDF, L("a5"), ("es", 0, 2048), L("a", 0, CB)], [ALL(RB)], ct(1280))
+            add("t", [lambda k=k: te.matmul(t[RB][:, 0:64], t.ew[:, 128 * k:128 * k + 128], x("m")[:, k::16], False, k == 15) for k in range(16)],
+                [("ew", 0, 2048), L("m", 0, CB)], [ALL(RB)], ct(1024))
+            add("v", lambda: v.tensor_scalar(x("pa")[:], t[RB][:, 0:64], float(THR - 17 * KB), None, ALU.is_ge), [ALL(RB)], [L("pa")], cv(64))
+            if st == 1:
+                add("t", lambda: te.matmul(t[QB][0:64, 136:144], x("pa")[:], t.bo[:, 0::16], True, True), [L("pa"), BO], [ALL(QB)], ct(64))
+                add("t", lambda: te.matmul(t[LX[1]][0:64, 0:128], x("pa")[:], t.bo[:], True, True), [L("pa"), BO], [ALL(LX[1])], ct(128))
+                add("s", lambda: sc.activation(x("f8")[0:64, :], t[QB][0:64, 128:144], AF.Relu, bias=t.bias[0:64, 0:1], accum_out=x("mm")[0:64, 0:1]),
+                    [ALL(QB), ("bias", 0, 1)], [L("f8", 0, 16), L("mm", 0, 1)], cv(64) + 0.02)
+                add("v", lambda: v.tensor_tensor(x("mk")[0:64, :], t.ml[0:64, :], t[LX[1]][0:64, 0:128], ALU.mult), [ALL(LX[1]), ("ml", 0, 128)], [L("mk", 0, 128)], cv(128))
+                add("v", lambda: v.tensor_copy(x("mn")[0:64, 0:1], x("mm")[0:64, 0:1]), [L("mm", 0, 1)], [L("mn", 0, 1)], cv(1))
+                add("v", lambda: v.tensor_scalar(x("od")[0:64, 0:1], x("mn")[0:64, 0:1], 1, None, ALU.bitwise_and), [L("mn", 0, 1)], [L("od", 0, 1)], cv(1))
+                add("v", lambda: v.tensor_scalar(t.mout[0:64, q0 + 64:q0 + 65], x("od")[0:64, 0:1], t.minb[0:64, o + 64:o + 65], 1.0, ALU.add, ALU.add),
+                    [L("od", 0, 1), ("minb", o + 64, o + 72)], [("mout", q0 + 64, q0 + 68)], cv(1))
+                add("v", lambda: v.tensor_scalar(x("rb")[0:64, :], t.e4s[0:64, :], t.mout[0:64, q0 + 64:q0 + 65], None, ALU.mult),
+                    [("mout", q0 + 64, q0 + 68), ("e4s", 0, 64)], [L("rb")], cv(64))
+                add("t", [lambda: te.matmul(t[LX[0]][:, 0:64], t.idf[:], t.ck[:], True, False),
+                          lambda: te.matmul(t[LX[0]][:, 0:64], x("mk")[0:64, :], t.e4n[0:64, :], False, False)],
+                    [IDF, CK, L("mk", 0, 128), ("e4n", 0, 64)], [ALL(LX[0])], ct(320))
+                add("t", lambda: te.matmul(t[LX[0]][:, 0:64], t.ml[0:64, :], x("rb")[0:64, :], False, True), [("ml", 0, 128), L("rb")], [ALL(LX[0])], ct(64))
+                add("v", lambda: v.tensor_tensor(x("ns")[:], MI.indirect(t.cl[:, 0:4]), U, ALU.not_equal), [MIR, ("cl", 0, 4), UR], [L("ns")], cg(64))
+                add("s", lambda: sc.activation(x("se")[:], x("ns")[:], AF.Copy, bias=1.0, scale=-1.0), [L("ns")], [L("se")], cv(64))
+                add("v", lambda: v.tensor_tensor(x("ua")[:], x("ns")[:], U, ALU.mult), [L("ns"), UR], [L("ua")], cv(128))
+                if s < N - 1:
+                    for j in range(4):
+                        add("v", lambda j=j: v.tensor_reduce(x("mo")[:, j:j + 1], x("ua")[:, j:64:4], AxisListType.X, ALU.max), [L("ua")], [L("mo", j, j + 1)], cv(16))
+                    add("v", lambda: v.tensor_tensor(x("lk")[:], x("li")[:], t.ckd[:], ALU.add), [L("li", 0, 4), ("ckd", 0, 4)], [L("lk", 0, 4)], cv(4))
+                    add("v", lambda: v.tensor_tensor(x("nk")[:], x("lk")[:], t[LX[0]][:, 0:4], ALU.add), [L("lk", 0, 4), ALL(LX[0])], [L("nk", 0, 4)], cv(4))
+                    add("v", lambda: v.tensor_tensor(t.mxo[:, k0:k0 + 4], x("nk")[:], x("mo")[:], ALU.max), [L("nk", 0, 4), L("mo", 0, 4)], [("mxo", k0, k0 + 4)], cv(8))
+                    k1, ks = k0 + 8 * NB, "k%d_%d" % (s + 1, b)
+                    snd = add("g", lambda: g.remote_dma(t.mia[:, k1:k1 + 4], t.mxo[:, k0:k0 + 4], t.sem[ks], t.sem.lsem, npid, nrid, nmask),
+                              [("mxo", k0, k0 + 4)], (), 1.0, "lsem", -nne)
+                    add("r", [], (), [("mia", k1, k1 + 4)], HOP, ks, nne, (snd,))
+                add("v", lambda: v.tensor_tensor(t[LX[0]][:, 64:128], x("se")[:], t[LX[0]][:, 0:64], ALU.mult), [L("se"), ALL(LX[0])], [ALL(LX[0])], cv(64))
+                add("v", lambda: v.tensor_tensor(t.mout[:, q0:q0 + 64], t[LX[0]][:, 64:128], x("ua")[:], ALU.add), [ALL(LX[0]), L("ua")], [("mout", q0, q0 + 64)], cv(64))
+                add("t", [lambda: te.matmul(t[LX[1]][0:64, 128:136], t.idf[0:64, 0:64], t.minb[0:64, o + 72:o + 80], True, False)] +
+                    [lambda k=k: te.matmul(t[LX[1]][0:64, 128:136], t.idb[0:64, 0:64], x("f8")[0:64, 8 * k:8 * k + 8], False, k == 1) for k in range(2)],
+                    [IDF, IDB, ("minb", o + 72, o + 80), L("f8", 0, 16)], [ALL(LX[1])], ct(384))
+                add("s", lambda: sc.activation(t.mout[0:64, q0 + 72:q0 + 80], t[LX[1]][0:64, 128:136], AF.Copy), [ALL(LX[1])], [("mout", q0 + 72, q0 + 80)], cv(64))
+                hs, no = "h%d_%d" % (s + 1, b), mi(s + 1, b)
+                snd = add("g", lambda: g.remote_dma(t.minb[:, no:no + MW], t.mout[:, q0:q0 + MW], t.sem[hs], t.sem.lsem, npid, nrid, nmask),
+                          [("mout", q0, q0 + MW)], (), 1.0, "lsem", -nne)
+                add("r", [], (), [("minb", no, no + MW)], HOP + 0.5, hs, nne, (snd,))
+            BK, q1 = (QB, 0) if st == 0 else (RB, 64)
+            add("t", [lambda BK=BK, q1=q1: te.matmul(t[BK][:, q1:q1 + 64], t.idf[:], x("cf")[:], True, False),
+                      lambda BK=BK, q1=q1: te.matmul(t[BK][:, q1:q1 + 64], t.bq[:], x("pa")[:], False, True)],
+                [IDF, L("cf"), ("bq", 0, 128), L("pa")], [ALL(BK)], ct(320))
+            add("v", lambda BK=BK, q1=q1: v.tensor_tensor(x("bm")[:], x("ax")[:], t[BK][:, q1:q1 + 64], ALU.min), [L("ax"), ALL(BK)], [L("bm")], cv(64))
+            add("v", lambda: v.tensor_tensor(x("yi")[:], x("bm")[:], t[RB][:, 0:64], ALU.min), [L("bm"), ALL(RB)], [L("yi")], cv(64))
+            add("v", lambda: v.tensor_scalar(x("ci")[:], x("yi")[:], 4095, None, ALU.bitwise_and), [L("yi")], [L("ci")], cv(64))
+            if st == 0:
+                add("v", lambda: v.tensor_copy(x("co")[:], x("ci")[:]), [L("ci")], [L("co")], cv(64))
+                add("t", lambda: te.matmul(t[QB][0:64, 128:136], x("pa")[:], t.bo[:, 0::16], True, True), [L("pa"), BO], [ALL(QB)], ct(64))
+            else:
+                add("v", lambda: v.tensor_copy(t.cw[:, cs:ce].indirect(x("ls")[:, 0:4]), x("ci")[:]), [L("ci"), L("ls", 0, 4)], [("cw", cs, ce)], (0.05 + 3.8 * 64 * CYC) * FAC)
+        if s == N - 1:
+            add("y", lambda: g.sync.dma_start(t.yg[:, cs:ce], t.cw[:, cs:ce]), [("cw", cs, ce)], (), 0.06, nm("oyg", b), 16, (), 4.0)
+
+    for s in range(N):
+        for b in range(NB):
+            cur[0] = BON * b
+            slice_block(s, b)
+    cur[0] = 0.0
+
+    for b in range(NB):
+        o = mi(N, b)
+        L0, L1 = nm("pb", 2 * b), nm("pb", 2 * b + 1)
+        x = lambda n, b=b: t[nm(n, b)]
+        add("s", lambda o=o, x=x: sc.activation(x("rb")[0:64, :], t.e4[0:64, :], AF.Identity, scale=t.minb[0:64, o + 64:o + 65]), [("e4", 0, 64), ("minb", o + 64, o + 72)], [(nm("rb", b), 0, 64)], cv(64))
+        add("t", [lambda o=o, L0=L0: te.matmul(t[L0][0:64, 0:128], t.minb[:, o:o + 64], t.idp[:], True, False),
+                  lambda L0=L0: te.matmul(t[L0][0:64, 0:128], t.ck[:], t.idn[:], False, False),
+                  lambda L0=L0, x=x: te.matmul(t[L0][0:64, 0:128], x("rb")[0:64, :], t.ml[0:64, :], False, True)],
+            [("minb", o, o + 64), ("idn", 0, 128), CK, ("idp", 0, 128), (nm("rb", b), 0, 64), ("ml", 0, 128)], [(L0, 0, 512)], ct(1152))
+        add("v", lambda L0=L0, x=x: v.tensor_copy(x("vo")[0:64, :], t[L0][0:64, 0:128]), [(L0, 0, 512)], [(nm("vo", b), 0, 128)], cv(128))
+        for (q, k0) in (("y", 0), ("s", 4)):
+            add(q, [lambda b=b, k=k, q=q, x=x: eng[q].dma_start(t.yv[16 * k:16 * k + 16, 64 * b:64 * b + 64], x("vo")[0:64, 16 * k:16 * k + 16]) for k in range(k0, k0 + 4)],
+                [(nm("vo", b), 0, 128)], (), 0.24, nm("oyv", b), 64 if q == "y" else 128, (), 2.0)
+        add("t", lambda o=o, L1=L1: te.matmul(t[L1][0:8, 0:64], t.minb[0:64, o + 72:o + 80], t.idf[0:64, 0:64], True, True), [("minb", o + 72, o + 80), IDF], [(L1, 0, 512)], ct(256))
+        add("s", lambda L1=L1, x=x: sc.activation(x("yo")[0:8, :], t[L1][0:8, 0:64], AF.Copy), [(L1, 0, 512)], [(nm("yo", b), 0, 64)], cv(64))
+        add("y", lambda b=b, x=x: g.sync.dma_start(t.ym[:, 64 * b:64 * b + 64], x("yo")[0:8, :]), [(nm("yo", b), 0, 64)], (), 0.06, nm("oym", b), 16, (), 2.0)
+
+    order = schedule(nodes)
+    pos = {i: k for k, i in enumerate(order)}
+    cnt, known, tok, total = {}, {q: {} for q in eng}, {}, {}
+    for i in order:
+        d = nodes[i]
+        q = d["q"]
+        if q == "r":
+            tok[i] = (d["sem"], d["val"], {})
+            total[d["sem"]] = d["val"]
+            continue
+        kn = known[q]
+        for j in sorted(d["dep"], key=lambda j: -pos[j]):
+            if not d["dep"][j]:
+                continue
+            sem, val, jk = tok[j]
+            if kn.get(sem, 0) >= val:
+                continue
+            eng[q].wait_ge(t.sem[sem], val)
+            for (a, w) in list(jk.items()) + [(sem, val)]:
+                kn[a] = max(kn.get(a, 0), w)
+        ins = None
+        for f in d["f"]:
+            ins = f()
+            if d["sem"] and d["val"] > 0:
+                ins.then_inc(t.sem[d["sem"]], 16)
+        if d["sem"] is None:
+            sem = csem[q]
+            cnt[sem] = cnt.get(sem, 0) + 1
+            ins.then_inc(t.sem[sem], 1)
+            tok[i] = (sem, cnt[sem], dict(kn))
+            total[sem] = cnt[sem]
+        elif d["val"] > 0:
+            tok[i] = (d["sem"], d["val"], dict(kn))
+            total[d["sem"]] = max(d["val"], total.get(d["sem"], 0))
+        else:
+            total[d["sem"]] = total.get(d["sem"], 0) - d["val"]
+    for sem in total:
+        if known["g"].get(sem, 0) < total[sem]:
+            g.wait_ge(t.sem[sem], total[sem])

@@ -1,12 +1,15 @@
 from concourse.bass import DstId, RemoteDMATransfer
 from concourse.mybir import AluOpType as ALU, AxisListType, ActivationFunctionType as AF
 
-N, NB, LB, NS = 8, 2, 64, 4
-LS = LB // NS
+N, NB = 8, 2
+LB = 128 // NB
+H = LB // 16
+LS = 16
+NS = LB // LS
 CB, CS = 16 * LB, 16 * LS
-MW = 80
-GS = ((1, 3),)
-BON, LOOK = 3.0, 0.1
+MW = LB + 16
+GS = ((1, NS - 1),)
+BON, LOOK, HOLD = 3.0, 0.1, 0.4
 KB = 1 << 19
 W15 = 1 << 15
 THR = 10 * W15
@@ -27,21 +30,17 @@ SCRATCH = {
     "pmt": ("sbuf", [128, 128], "bfloat16"), "es": ("sbuf", [128, 2048], "bfloat16"), "ew": ("sbuf", [128, 2048], "bfloat16"),
     "ex": ("sbuf", [128, 2048], "bfloat16"),
     "ix": ("sbuf", [128, 128], "int32"), "ix2": ("sbuf", [128, 128], "int32"), "ml": ("sbuf", [128, 128], "bfloat16"),
-    "ka": ("sbuf", [128, 64], "int32"), "ka2": ("sbuf", [128, 64], "int32"), "kb": ("sbuf", [128, 64], "int32"), "ck": ("sbuf", [128, 64], "float32"),
-    "ckd": ("sbuf", [128, 4], "float32"), "r16": ("sbuf", [128, 64], "bfloat16"),
-    "cli": ("sbuf", [128, 4], "int32"), "cli2": ("sbuf", [128, 4], "int32"), "cl": ("sbuf", [128, 4], "uint16"),
-    "e4a": ("sbuf", [128, 64], "bfloat16"), "e4": ("sbuf", [128, 64], "bfloat16"), "e4s": ("sbuf", [128, 64], "bfloat16"), "e4n": ("sbuf", [128, 64], "bfloat16"),
+    "ka": ("sbuf", [128, LB], "int32"), "ka2": ("sbuf", [128, LB], "int32"), "kb": ("sbuf", [128, LB], "int32"), "ck": ("sbuf", [128, LB], "float32"),
+    "r16": ("sbuf", [128, LB], "bfloat16"), "cli": ("sbuf", [128, H], "int32"), "cli2": ("sbuf", [128, H], "int32"), "cl": ("sbuf", [128, H], "uint16"),
+    "e4a": ("sbuf", [128, LB], "bfloat16"), "e4": ("sbuf", [128, LB], "bfloat16"), "e4s": ("sbuf", [128, LB], "bfloat16"), "e4n": ("sbuf", [128, LB], "bfloat16"),
 }
-for _b in range(NB):
-    for _n, _c, _d in (("f", CB, "bfloat16"), ("gq", CB, "bfloat16"), ("a", CB, "bfloat16"), ("m", CB, "bfloat16"),
-                       ("li", 4, "int32"), ("ls", 4, "uint16"), ("cf", 64, "float32"), ("co", 64, "uint16"),
-                       ("lk", 4, "float32"), ("mo", 4, "float32"), ("nk", 4, "float32"),
-                       ("pg_", 64, "bfloat16"), ("po", 64, "uint16"), ("a5", 64, "float32"), ("ax", 64, "float32"),
-                       ("pa", 64, "bfloat16"), ("bm", 64, "float32"), ("yi", 64, "int32"), ("ci", 64, "int32"),
-                       ("f8", 16, "bfloat16"), ("mm", 4, "float32"), ("mn", 4, "int32"), ("od", 4, "int32"), ("rb", 64, "bfloat16"),
-                       ("mk", 128, "bfloat16"), ("ns", 64, "float32"), ("se", 64, "float32"), ("ua", 64, "float32"),
-                       ("vo", 128, "float32"), ("yo", 64, "float32")):
-        SCRATCH["%s%d" % (_n, _b)] = ("sbuf", [128, _c], _d)
+TILE = {"f": (CB, "bfloat16"), "gq": (CB, "bfloat16"), "a": (CB, "bfloat16"), "m": (CB, "bfloat16"), "li": (4, "int32"), "ls": (4, "uint16"),
+        "cf": (LB, "float32"), "co": (LB, "uint16"), "lk": (4, "float32"), "mo": (4, "float32"), "pg_": (LB, "bfloat16"), "po": (LB, "uint16"),
+        "a5": (LB, "float32"), "ax": (LB, "float32"), "pa": (LB, "bfloat16"), "bm": (LB, "float32"), "yi": (LB, "int32"), "ci": (LB, "int32"),
+        "f8": (16, "bfloat16"), "mm": (4, "float32"), "mn": (4, "int32"), "od": (4, "int32"), "rb": (LB, "bfloat16"), "mk": (128, "bfloat16"),
+        "ns": (LB, "float32"), "se": (LB, "float32"), "ua": (LB, "float32"), "vo": (128, "float32"), "yo": (LB, "float32")}
+for _n in TILE:
+    SCRATCH[_n] = ("sbuf", [128, NB * TILE[_n][0]], TILE[_n][1])
 for _b in range(8):
     SCRATCH["pb%d" % _b] = ("psum", [128, 512], "float32")
 
@@ -49,7 +48,7 @@ SEMAPHORES = ["qv", "qs", "qt", "qg", "lsem", "limr", "dlim", "dvv", "dxt"]
 SEMAPHORES += ["%s%d" % (n, b) for n in ("dpg", "dpre", "oyg", "oyv", "oym") for b in range(NB)]
 SEMAPHORES += ["h%d_%d" % (s, b) for s in range(1, N + 1) for b in range(NB)] + ["k%d_%d" % (s, b) for s in range(1, N) for b in range(NB)]
 
-CYC, FAC, WAKE, XG, PEC, HOP = 0.00083, 1.25, 0.1, 1.56, 0.0005, 2.0
+CYC, FAC, WAKE, XG, PEC, HOP = 0.00083, 1.0, 0.2, 1.56, 0.0004, 4.0
 
 
 def cv(n):
@@ -92,6 +91,8 @@ def schedule(nodes):
             f = free.get(q, 0.0)
             t0 = min(max(f, ready[i]) for i in pool[q])
             i = max((i for i in pool[q] if max(f, ready[i]) <= t0 + LOOK), key=lambda i: pri[i])
+            e0 = max(f, ready[i]) + HOLD * nodes[i]["c"]
+            i = max((j for j in pool[q] if ready[j] <= e0), key=lambda j: pri[j])
             st = max(f, ready[i])
             if best is None or st < best[0]:
                 best = (st, q, i)
@@ -117,6 +118,7 @@ def rank_program(g, core, T, topo):
     eng = {"v": g.vector, "s": g.scalar, "t": g.tensor, "g": g, "y": g.sync}
     csem = {"v": "qv", "s": "qs", "t": "qt", "g": "qg"}
     nodes, last, cur = [], {}, [0.0]
+    STREAM = ("ls", "co", "po", "cw", "f")
 
     def add(q, fns, R=(), W=(), c=0.08, sem=None, val=None, after=(), lat=0.0):
         i = len(nodes)
@@ -131,7 +133,7 @@ def rank_program(g, core, T, topo):
                     same = nodes[j]["q"] == q
                     if not (wr or jw) and (same or not bank):
                         continue
-                    need = not (same and (q == "t" or not jw))
+                    need = not (same and (q == "t" or not (jw or buf in STREAM)))
                     dep[j] = dep.get(j, False) or need
                 if wr:
                     if bank and q == "t":
@@ -147,18 +149,17 @@ def rank_program(g, core, T, topo):
     t = T
     nm = lambda n, b: "%s%d" % (n, b)
     v, sc, te = g.vector, g.scalar, g.tensor
-    IDF, CK, IDB, NID, BO = ("idf", 0, 128), ("ck", 0, 64), ("idb", 0, 128), ("nid", 0, 128), ("bo", 0, 128)
+    IDF, CK, IDB, NID, BO, ML, E4 = ("idf", 0, 128), ("ck", 0, LB), ("idb", 0, 128), ("nid", 0, 128), ("bo", 0, 128), ("ml", 0, 128), ("e4", 0, LB)
 
     def load(fns, W, sem, cost, q="y"):
         add(q, fns, (), W, 0.06 * len(fns), sem, 16 * len(fns), (), cost)
     load([lambda k=k: g.scalar.dma_start(t.vt[:, 16 * k:16 * k + 16], t.vv[16 * k:16 * k + 16, :]) for k in range(8)], [("vt", 0, 128)], "dvv", 3.0, "s")
+    load([lambda: g.sync.dma_start(t.limo[:], t.lim[:])], [("limo", 0, 128)], "dlim", 2.5)
     for b in range(NB):
-        load([lambda b=b: g.sync.dma_start(t.pgi[:, CB * b:CB * b + CB], t.pg[:, CB * b:CB * b + CB])], [("pgi", CB * b, CB * b + CB)], nm("dpg", b), 4.0 + 4 * b)
+        load([lambda b=b: g.sync.dma_start(t.pgi[:, CB * b:CB * b + CB], t.pg[:, CB * b:CB * b + CB])], [("pgi", CB * b, CB * b + CB)], nm("dpg", b), 4.5 + 5.5 * b)
         if b == 0:
-            load([lambda: g.sync.dma_start(t.xw[:], t.xt[:])], [("xw", 0, 4096)], "dxt", 6.5)
-        load([lambda b=b: g.sync.dma_start(t.pw[:, CB * b:CB * b + CB], t.pre[:, CB * b:CB * b + CB])], [("pw", CB * b, CB * b + CB)], nm("dpre", b), 7.0 + 2 * b)
-        if b == 0:
-            load([lambda: g.sync.dma_start(t.limo[:], t.lim[:])], [("limo", 0, 128)], "dlim", 7.5)
+            load([lambda: g.sync.dma_start(t.xw[:], t.xt[:])], [("xw", 0, 4096)], "dxt", 7.0)
+        load([lambda b=b: g.sync.dma_start(t.pw[:, CB * b:CB * b + CB], t.pre[:, CB * b:CB * b + CB])], [("pw", CB * b, CB * b + CB)], nm("dpre", b), 7.5 + 4.0 * b)
 
     def vmem(buf, a, b, val):
         add("v", lambda: v.memset(t[buf][:, a:b], val), (), [(buf, a, b)], cv((b - a) * (0.5 if SCRATCH[buf][2] == "bfloat16" else 1)))
@@ -173,25 +174,24 @@ def rank_program(g, core, T, topo):
     vmem("posb", 0, 128, 1024.0)
     vmem("bias", 0, 1, -15.0)
     gen("idf", 128, lambda: g.affine_select(t.idf[:], t.onef[:], [[-1, 128]], ALU.is_equal, 0.0, 0, 1), "onef")
-    gen("pmt", 128, lambda: g.affine_select(t.pmt[:], t.posb[:], [[-4, 2], [-8, 16], [-1, 4]], ALU.is_equal, 0.0, 0, 1), "posb")
-    gen("ka", 64, lambda: g.iota(t.ka[:], [[0, 64]], 0, 16))
-    gen("kb", 64, lambda: g.iota(t.kb[:], [[-1, 16], [-256, 4]], 65536 + 1023, 0))
-    gen("cli", 4, lambda: g.iota(t.cli[:], [[0, 4]], 0, 1))
-    gen("r16", 64, lambda: g.iota(t.r16[:], [[0, NS], [16, LS]], 0, 0, allow_small_or_imprecise_dtypes=True))
+    gen("pmt", 128, lambda: g.affine_select(t.pmt[:], t.posb[:], [[-H, NB], [-8, 16], [-1, H]], ALU.is_equal, 0.0, 0, 1), "posb")
+    gen("ka", LB, lambda: g.iota(t.ka[:], [[0, LB]], 0, 16))
+    gen("kb", LB, lambda: g.iota(t.kb[:], [[-1, 16], [-256, H]], 65536 + 1023, 0))
+    gen("cli", H, lambda: g.iota(t.cli[:], [[0, H]], 0, 1))
+    gen("r16", LB, lambda: g.iota(t.r16[:], [[0, NS], [16, LS]], 0, 0, allow_small_or_imprecise_dtypes=True))
     gen("bo0", 128, lambda: g.affine_select(t.bo0[:], t.oneb[:], [[-16, 8], [0, 16]], ALU.is_ge, 0.0, 0, 1), "oneb")
     gen("bo", 128, lambda: g.affine_select(t.bo[:], t.bo0[:], [[16, 8], [0, 16]], ALU.is_ge, 0.0, 15, -1), "bo0")
     gen("es", 2048, lambda: g.iota(t.es[:], [[0, 2048]], 0, 0, allow_small_or_imprecise_dtypes=True))
     gen("ix", 128, lambda: g.iota(t.ix[:], [[-1, 128]], 128, 1))
-    gen("e4a", 64, lambda: g.affine_select(t.e4a[:], t.oneb[:, 0:64], [[0, 16], [-16, 4]], ALU.is_ge, 0.0, 0, 1), "oneb")
-    gen("e4", 64, lambda: g.affine_select(t.e4[:], t.e4a[:], [[0, 16], [16, 4]], ALU.is_ge, 0.0, 15, -1), "e4a")
+    gen("e4a", LB, lambda: g.affine_select(t.e4a[:], t.oneb[:, 0:LB], [[0, 16], [-16, H]], ALU.is_ge, 0.0, 0, 1), "oneb")
+    gen("e4", LB, lambda: g.affine_select(t.e4[:], t.e4a[:], [[0, 16], [16, H]], ALU.is_ge, 0.0, 15, -1), "e4a")
     gen("mout", MW * NB * N, lambda: g.iota(t.mout[:], [[0, MW * NB * N]], 0, 0, allow_small_or_imprecise_dtypes=True))
     vts("idb", "idf", 128, lambda: v.tensor_copy(t.idb[:], t.idf[:]))
     add("v", lambda: v.tensor_copy(t.vtb[:], t.vt[:]), [("vt", 0, 128)], [("vtb", 0, 128)], cv(128))
-    vts("ka2", "ka", 64, lambda: v.tensor_scalar(t.ka2[:], t.ka[:], 255, None, ALU.bitwise_and))
-    add("v", lambda: v.tensor_tensor(t.ck[:], t.kb[:], t.ka2[:], ALU.subtract), [("ka2", 0, 64), ("kb", 0, 64)], [CK], cv(128))
-    vts("cli2", "cli", 4, lambda: v.tensor_scalar(t.cli2[:], t.cli[:], 3, None, ALU.bitwise_and))
-    vts("cl", "cli2", 4, lambda: v.tensor_copy(t.cl[:], t.cli2[:]))
-    add("v", lambda: v.tensor_scalar(t.ckd[:], t.ck[:, 0:4], -1.0, 65536.0, ALU.mult, ALU.add), [CK], [("ckd", 0, 4)], cv(4))
+    vts("ka2", "ka", LB, lambda: v.tensor_scalar(t.ka2[:], t.ka[:], 255, None, ALU.bitwise_and))
+    add("v", lambda: v.tensor_tensor(t.ck[:], t.kb[:], t.ka2[:], ALU.subtract), [("ka2", 0, LB), ("kb", 0, LB)], [CK], cv(2 * LB))
+    vts("cli2", "cli", H, lambda: v.tensor_scalar(t.cli2[:], t.cli[:], H - 1, None, ALU.bitwise_and))
+    vts("cl", "cli2", H, lambda: v.tensor_copy(t.cl[:], t.cli2[:]))
     for b in range(NB):
         add("v", lambda b=b: v.tensor_copy(t.cw[:, CB * b:CB * b + CB], t.pgi[:, CB * b:CB * b + CB]), [("pgi", CB * b, CB * b + CB)], [("cw", CB * b, CB * b + CB)], cv(CB))
 
@@ -200,15 +200,15 @@ def rank_program(g, core, T, topo):
     for b in range(NB):
         o = mi(0, b)
         pb = nm("pb", 6 + b)
-        add("t", [lambda b=b, pb=pb: te.matmul(t[pb][:, 448:512], t.vtb[:], t.pmt[:, 64 * b:64 * b + 64], True, True)],
+        add("t", [lambda b=b, pb=pb: te.matmul(t[pb][:, 448:448 + LB], t.vtb[:], t.pmt[:, LB * b:LB * b + LB], True, True)],
             [("vtb", 0, 128), ("pmt", 0, 128)], [(pb, 0, 512)], ct(64))
-        add("v", lambda o=o, pb=pb: v.tensor_tensor(t.minb[:, o:o + 64], t.ck[:], t[pb][:, 448:512], ALU.add), [(pb, 0, 512), CK], [("minb", o, o + 64)], cv(64))
-        vmem("minb", o + 64, o + 80, 0.0)
-        for j in range(4):
-            add("v", lambda j=j, b=b, o=o: v.tensor_reduce(t.mia[:, 8 * b + j:8 * b + j + 1], t.minb[:, o + j:o + 64:4], AxisListType.X, ALU.max),
-                [("minb", o, o + 64)], [("mia", 8 * b + j, 8 * b + j + 1)], cv(16))
-    add("t", lambda: te.matmul(t.pb4[:, 0:128], t.limo[:], t.idb[:], True, True), [("limo", 0, 128), IDB], [("pb4", 0, 512)], ct(128))
-    add("s", lambda: sc.activation(t.limt[:, 0:128], t.pb4[:, 0:128], AF.Copy), [("pb4", 0, 512)], [("limt", 0, 128)], cv(128))
+        add("v", lambda o=o, pb=pb: v.tensor_tensor(t.minb[:, o:o + LB], t.ck[:], t[pb][:, 448:448 + LB], ALU.add), [(pb, 0, 512), CK], [("minb", o, o + LB)], cv(LB))
+        vmem("minb", o + LB, o + MW, 0.0)
+        for j in range(H):
+            add("v", lambda j=j, b=b, o=o: v.tensor_reduce(t.mia[:, 8 * b + j:8 * b + j + 1], t.minb[:, o + j:o + LB:H], AxisListType.X, ALU.max),
+                [("minb", o, o + LB)], [("mia", 8 * b + j, 8 * b + j + 1)], cv(16))
+    add("t", lambda: te.matmul(t.pb0[:, 0:128], t.limo[:], t.idb[:], True, True), [("limo", 0, 128), IDB], [("pb0", 0, 512)], ct(128))
+    add("s", lambda: sc.activation(t.limt[:, 0:128], t.pb0[:, 0:128], AF.Copy), [("pb0", 0, 512)], [("limt", 0, 128)], cv(128))
     nxt = T.cores[(rank + 1) % N]
     nrid, npid, _ = topo.addr(nxt)
     nmask = topo.mask(core, nxt)
@@ -236,113 +236,142 @@ def rank_program(g, core, T, topo):
     vts("nid", "idb", 128, lambda: v.tensor_scalar(t.nid[:], t.idb[:], -1.0, None, ALU.mult), True)
     vts("ix2", "ix", 128, lambda: v.tensor_scalar(t.ix2[:], t.ix[:], 15, None, ALU.bitwise_and))
     vts("ml", "ix2", 128, lambda: v.tensor_scalar(t.ml[:], t.ix2[:], 0.0, None, ALU.is_equal))
-    vts("e4s", "e4", 64, lambda: v.tensor_scalar(t.e4s[:], t.e4[:], -1024.0, None, ALU.mult), True)
-    vts("e4n", "e4", 64, lambda: v.tensor_scalar(t.e4n[:], t.e4[:], 1024.0, None, ALU.mult), True)
+    vts("e4s", "e4", LB, lambda: v.tensor_scalar(t.e4s[:], t.e4[:], -1024.0, None, ALU.mult), True)
+    vts("e4n", "e4", LB, lambda: v.tensor_scalar(t.e4n[:], t.e4[:], 1024.0, None, ALU.mult), True)
     vts("idp", "idf", 128, lambda: v.tensor_scalar(t.idp[:], t.idf[:], 1.0 / 1024, None, ALU.mult))
     vts("idn", "idf", 128, lambda: v.tensor_scalar(t.idn[:], t.idf[:], -1.0 / 1024, None, ALU.mult))
 
-    def slice_block(s, b):
-        o, q0 = mi(s, b), MW * (NB * s + b)
-        L = lambda n, a=0, e=64: (nm(n, b), a, e)
-        x = lambda n: t[nm(n, b)]
-        U, UR = t.minb[:, o:o + 64], ("minb", o, o + 64)
-        cs, ce = CB * b, CB * b + CB
-        LX, RB, QB = [nm("pb", 2 * b), nm("pb", 2 * b + 1)], nm("pb", 4 + b), nm("pb", 6 + b)
-        ALL = lambda bank: (bank, 0, 512)
-        k0 = 8 * (NB * s + b)
-        MI, MIR = t.mia[:, k0:k0 + 4], ("mia", k0, k0 + 4)
-        add("v", lambda: v.tensor_scalar(x("li")[:, 0:4], MI, 1023, None, ALU.bitwise_and), [MIR], [L("li", 0, 4)], cv(4))
-        add("v", lambda: v.tensor_scalar(x("ls")[:, 0:4], x("li")[:, 0:4], -1.0, 1023.0, ALU.mult, ALU.add), [L("li", 0, 4)], [L("ls", 0, 4)], cv(4))
-        add("s", lambda: sc.activation(x("cf")[:], t.cw[:, cs:ce].indirect(x("ls")[:, 0:4]), AF.Copy), [("cw", cs, ce), L("ls", 0, 4)], [L("cf")], cg(64))
-        add("v", lambda: v.tensor_copy(x("co")[:], x("cf")[:]), [L("cf")], [L("co")], cv(64))
-        add("s", lambda: sc.activation(x("pg_")[:], t.pw[:, cs:ce].indirect(x("ls")[:, 0:4]), AF.Copy), [("pw", cs, ce), L("ls", 0, 4)], [L("pg_")], cg(64))
-        add("t", [lambda: te.matmul(t[QB][:, 64:128], t.idb[:], x("pg_")[:], True, False), lambda: te.matmul(t[QB][:, 64:128], t.idb[:], t.r16[:], False, True)],
-            [IDB, L("pg_"), ("r16", 0, 64)], [ALL(QB)], ct(128))
-        add("v", lambda: v.tensor_copy(x("po")[:], t[QB][:, 64:128]), [ALL(QB)], [L("po")], cv(64))
-        for st in range(2):
-            if st == 0:
-                for h in range(2):
-                    add("t", lambda h=h: te.matmul(t[LX[h]][:], t.limt[:, 128 * s:128 * s + 128], t.ex[:, cs + 512 * h:cs + 512 * h + 512], True, True),
-                        [("limt", 128 * s, 128 * s + 128), ("ex", 0, 2048)], [ALL(LX[h])], ct(512))
-            else:
-                add("v", lambda: v.tensor_copy(x("cf")[:], x("ci")[:]), [L("ci")], [L("cf")], cv(64))
+    def tiles(b):
+        def L(n, a=0, e=None):
+            w = TILE[n][0]
+            return (n, w * b + a, w * b + (w if e is None else e))
 
-            def piece(u):
-                p0, p1, l0, l1 = CS * u, CS * u + CS, LS * u, LS * u + LS
-                lb, c0, DB = LX[p0 // 512], p0 % 512, (QB, RB)[u % 2]
-                f, gq, a, m = [x(n)[:, p0:p1] for n in ("f", "gq", "a", "m")]
-                win = lambda: x("f")[:, p0:p1].indirect(x("po")[:, l0:l1])
-                add("s", lambda: sc.activation(f, t.xw[:].indirect(x("co")[:, l0:l1]), AF.Copy), [("xw", 0, 4096), L("co", l0, l1)], [L("f", p0, p1)], cg(CS))
-                gio = [L("f", p0, p1), L("po", l0, l1)], [L("gq", p0, p1)], cg(CS)
-                if (st, u) in GS:
-                    add("s", lambda: sc.activation(gq, win(), AF.Copy), *gio)
-                else:
-                    add("v", lambda: v.tensor_copy(gq, win()), *gio)
-                add("t", [lambda: te.matmul(t[DB][:, 192:192 + CS], t.idb[:], f, True, False), lambda: te.matmul(t[DB][:, 192:192 + CS], t.nid[:], gq, False, True)],
-                    [IDB, NID, L("f", p0, p1), L("gq", p0, p1)], [ALL(DB)], ct(2 * CS))
-                add("s", lambda: sc.activation(a, t[DB][:, 192:192 + CS], AF.Abs), [ALL(DB)], [L("a", p0, p1)], cv(CS))
-                add("v", lambda: v.tensor_tensor(m, a, t[lb][:, c0:c0 + CS], ALU.is_le), [L("a", p0, p1), ALL(lb)], [L("m", p0, p1)], cv(CS))
-            for u in range(NS):
-                piece(u)
-            add("s", lambda: sc.activation(x("a5")[:], x("cf")[:], AF.Copy, bias=float(1 - 17 * KB), scale=5.0), [L("cf")], [L("a5")], cv(64))
-            add("s", lambda: sc.activation(x("ax")[:], x("cf")[:], AF.Copy, bias=float(1 - 17 * KB + THR), scale=5.0), [L("cf")], [L("ax")], cv(64))
-            add("t", [lambda: te.matmul(t[RB][:, 0:64], t.idf[:], x("a5")[:], True, False)] +
-                [lambda k=k: te.matmul(t[RB][:, 0:64], t.es[:, 128 * k:128 * k + 128], x("a")[:, k::16], False, False) for k in range(16)],
-                [IDF, L("a5"), ("es", 0, 2048), L("a", 0, CB)], [ALL(RB)], ct(1280))
-            add("t", [lambda k=k: te.matmul(t[RB][:, 0:64], t.ew[:, 128 * k:128 * k + 128], x("m")[:, k::16], False, k == 15) for k in range(16)],
-                [("ew", 0, 2048), L("m", 0, CB)], [ALL(RB)], ct(1024))
-            add("v", lambda: v.tensor_scalar(x("pa")[:], t[RB][:, 0:64], float(THR - 17 * KB), None, ALU.is_ge), [ALL(RB)], [L("pa")], cv(64))
-            if st == 1:
-                add("t", lambda: te.matmul(t[QB][0:64, 136:144], x("pa")[:], t.bo[:, 0::16], True, True), [L("pa"), BO], [ALL(QB)], ct(64))
-                add("t", lambda: te.matmul(t[LX[1]][0:64, 0:128], x("pa")[:], t.bo[:], True, True), [L("pa"), BO], [ALL(LX[1])], ct(128))
-                add("s", lambda: sc.activation(x("f8")[0:64, :], t[QB][0:64, 128:144], AF.Relu, bias=t.bias[0:64, 0:1], accum_out=x("mm")[0:64, 0:1]),
-                    [ALL(QB), ("bias", 0, 1)], [L("f8", 0, 16), L("mm", 0, 1)], cv(64) + 0.02)
-                add("v", lambda: v.tensor_tensor(x("mk")[0:64, :], t.ml[0:64, :], t[LX[1]][0:64, 0:128], ALU.mult), [ALL(LX[1]), ("ml", 0, 128)], [L("mk", 0, 128)], cv(128))
-                add("v", lambda: v.tensor_copy(x("mn")[0:64, 0:1], x("mm")[0:64, 0:1]), [L("mm", 0, 1)], [L("mn", 0, 1)], cv(1))
-                add("v", lambda: v.tensor_scalar(x("od")[0:64, 0:1], x("mn")[0:64, 0:1], 1, None, ALU.bitwise_and), [L("mn", 0, 1)], [L("od", 0, 1)], cv(1))
-                add("v", lambda: v.tensor_scalar(t.mout[0:64, q0 + 64:q0 + 65], x("od")[0:64, 0:1], t.minb[0:64, o + 64:o + 65], 1.0, ALU.add, ALU.add),
-                    [L("od", 0, 1), ("minb", o + 64, o + 72)], [("mout", q0 + 64, q0 + 68)], cv(1))
-                add("v", lambda: v.tensor_scalar(x("rb")[0:64, :], t.e4s[0:64, :], t.mout[0:64, q0 + 64:q0 + 65], None, ALU.mult),
-                    [("mout", q0 + 64, q0 + 68), ("e4s", 0, 64)], [L("rb")], cv(64))
-                add("t", [lambda: te.matmul(t[LX[0]][:, 0:64], t.idf[:], t.ck[:], True, False),
-                          lambda: te.matmul(t[LX[0]][:, 0:64], x("mk")[0:64, :], t.e4n[0:64, :], False, False)],
-                    [IDF, CK, L("mk", 0, 128), ("e4n", 0, 64)], [ALL(LX[0])], ct(320))
-                add("t", lambda: te.matmul(t[LX[0]][:, 0:64], t.ml[0:64, :], x("rb")[0:64, :], False, True), [("ml", 0, 128), L("rb")], [ALL(LX[0])], ct(64))
-                add("v", lambda: v.tensor_tensor(x("ns")[:], MI.indirect(t.cl[:, 0:4]), U, ALU.not_equal), [MIR, ("cl", 0, 4), UR], [L("ns")], cg(64))
-                add("s", lambda: sc.activation(x("se")[:], x("ns")[:], AF.Copy, bias=1.0, scale=-1.0), [L("ns")], [L("se")], cv(64))
-                add("v", lambda: v.tensor_tensor(x("ua")[:], x("ns")[:], U, ALU.mult), [L("ns"), UR], [L("ua")], cv(128))
-                if s < N - 1:
-                    for j in range(4):
-                        add("v", lambda j=j: v.tensor_reduce(x("mo")[:, j:j + 1], x("ua")[:, j:64:4], AxisListType.X, ALU.max), [L("ua")], [L("mo", j, j + 1)], cv(16))
-                    add("v", lambda: v.tensor_tensor(x("lk")[:], x("li")[:], t.ckd[:], ALU.add), [L("li", 0, 4), ("ckd", 0, 4)], [L("lk", 0, 4)], cv(4))
-                    add("v", lambda: v.tensor_tensor(x("nk")[:], x("lk")[:], t[LX[0]][:, 0:4], ALU.add), [L("lk", 0, 4), ALL(LX[0])], [L("nk", 0, 4)], cv(4))
-                    add("v", lambda: v.tensor_tensor(t.mxo[:, k0:k0 + 4], x("nk")[:], x("mo")[:], ALU.max), [L("nk", 0, 4), L("mo", 0, 4)], [("mxo", k0, k0 + 4)], cv(8))
-                    k1, ks = k0 + 8 * NB, "k%d_%d" % (s + 1, b)
-                    snd = add("g", lambda: g.remote_dma(t.mia[:, k1:k1 + 4], t.mxo[:, k0:k0 + 4], t.sem[ks], t.sem.lsem, npid, nrid, nmask),
-                              [("mxo", k0, k0 + 4)], (), 1.0, "lsem", -nne)
-                    add("r", [], (), [("mia", k1, k1 + 4)], HOP, ks, nne, (snd,))
-                add("v", lambda: v.tensor_tensor(t[LX[0]][:, 64:128], x("se")[:], t[LX[0]][:, 0:64], ALU.mult), [L("se"), ALL(LX[0])], [ALL(LX[0])], cv(64))
-                add("v", lambda: v.tensor_tensor(t.mout[:, q0:q0 + 64], t[LX[0]][:, 64:128], x("ua")[:], ALU.add), [ALL(LX[0]), L("ua")], [("mout", q0, q0 + 64)], cv(64))
-                add("t", [lambda: te.matmul(t[LX[1]][0:64, 128:136], t.idf[0:64, 0:64], t.minb[0:64, o + 72:o + 80], True, False)] +
-                    [lambda k=k: te.matmul(t[LX[1]][0:64, 128:136], t.idb[0:64, 0:64], x("f8")[0:64, 8 * k:8 * k + 8], False, k == 1) for k in range(2)],
-                    [IDF, IDB, ("minb", o + 72, o + 80), L("f8", 0, 16)], [ALL(LX[1])], ct(384))
-                add("s", lambda: sc.activation(t.mout[0:64, q0 + 72:q0 + 80], t[LX[1]][0:64, 128:136], AF.Copy), [ALL(LX[1])], [("mout", q0 + 72, q0 + 80)], cv(64))
-                hs, no = "h%d_%d" % (s + 1, b), mi(s + 1, b)
-                snd = add("g", lambda: g.remote_dma(t.minb[:, no:no + MW], t.mout[:, q0:q0 + MW], t.sem[hs], t.sem.lsem, npid, nrid, nmask),
-                          [("mout", q0, q0 + MW)], (), 1.0, "lsem", -nne)
-                add("r", [], (), [("minb", no, no + MW)], HOP + 0.5, hs, nne, (snd,))
-            BK, q1 = (QB, 0) if st == 0 else (RB, 64)
-            add("t", [lambda BK=BK, q1=q1: te.matmul(t[BK][:, q1:q1 + 64], t.idf[:], x("cf")[:], True, False),
-                      lambda BK=BK, q1=q1: te.matmul(t[BK][:, q1:q1 + 64], t.bq[:], x("pa")[:], False, True)],
-                [IDF, L("cf"), ("bq", 0, 128), L("pa")], [ALL(BK)], ct(320))
-            add("v", lambda BK=BK, q1=q1: v.tensor_tensor(x("bm")[:], x("ax")[:], t[BK][:, q1:q1 + 64], ALU.min), [L("ax"), ALL(BK)], [L("bm")], cv(64))
-            add("v", lambda: v.tensor_tensor(x("yi")[:], x("bm")[:], t[RB][:, 0:64], ALU.min), [L("bm"), ALL(RB)], [L("yi")], cv(64))
-            add("v", lambda: v.tensor_scalar(x("ci")[:], x("yi")[:], 4095, None, ALU.bitwise_and), [L("yi")], [L("ci")], cv(64))
-            if st == 0:
-                add("v", lambda: v.tensor_copy(x("co")[:], x("ci")[:]), [L("ci")], [L("co")], cv(64))
-                add("t", lambda: te.matmul(t[QB][0:64, 128:136], x("pa")[:], t.bo[:, 0::16], True, True), [L("pa"), BO], [ALL(QB)], ct(64))
+        def X(n, a=0, e=None, p=128, st=1):
+            _, c0, c1 = L(n, a, e)
+            return t[n][0:p, c0:c1:st] if st > 1 else t[n][0:p, c0:c1]
+        return L, X, [nm("pb", 2 * b), nm("pb", 2 * b + 1)], nm("pb", 4 + b), nm("pb", 6 + b)
+    ALL = lambda bank: (bank, 0, 512)
+
+    def slice_block(s, b):
+        L, X, LX, RB, QB = tiles(b)
+        o, q0 = mi(s, b), MW * (NB * s + b)
+        U, UR = t.minb[:, o:o + LB], ("minb", o, o + LB)
+        cs, ce = CB * b, CB * b + CB
+        k0 = 8 * (NB * s + b)
+        MI, MIR = t.mia[:, k0:k0 + H], ("mia", k0, k0 + H)
+        add("v", lambda: v.tensor_scalar(X("li", 0, H), MI, 1023, None, ALU.bitwise_and), [MIR], [L("li")], cv(H))
+        add("v", lambda: v.tensor_scalar(X("ls", 0, H), X("li", 0, H), -1.0, 1023.0, ALU.mult, ALU.add), [L("li")], [L("ls")], cv(H))
+        add("v", lambda: v.tensor_copy(X("co"), t.cw[:, cs:ce].indirect(X("ls", 0, H))), [("cw", cs, ce), L("ls")], [L("co")], cg(LB))
+        add("s", lambda: sc.activation(X("cf"), t.cw[:, cs:ce].indirect(X("ls", 0, H)), AF.Copy), [("cw", cs, ce), L("ls")], [L("cf")], cg(LB))
+        add("s", lambda: sc.activation(X("pg_"), t.pw[:, cs:ce].indirect(X("ls", 0, H)), AF.Copy), [("pw", cs, ce), L("ls")], [L("pg_")], cg(LB))
+        add("t", [lambda: te.matmul(t[QB][:, 64:64 + LB], t.idb[:], X("pg_"), True, False), lambda: te.matmul(t[QB][:, 64:64 + LB], t.idb[:], t.r16[:], False, True)],
+            [IDB, L("pg_"), ("r16", 0, LB)], [ALL(QB)], ct(128))
+        add("v", lambda: v.tensor_copy(X("po"), t[QB][:, 64:64 + LB]), [ALL(QB)], [L("po")], cv(LB))
+        for h in range(2):
+            add("t", lambda h=h: te.matmul(t[LX[h]][:], t.limt[:, 128 * s:128 * s + 128], t.ex[:, cs + 512 * h:cs + 512 * h + 512], True, True),
+                [("limt", 128 * s, 128 * s + 128), ("ex", 0, 2048)], [ALL(LX[h])], ct(512))
+
+        def piece(st, u):
+            p0, p1, l0, l1 = CS * u, CS * u + CS, LS * u, LS * u + LS
+            lb, c0, DB = LX[p0 // 512], p0 % 512, (QB, RB)[u % 2]
+            win = lambda: X("f", p0, p1).indirect(X("po", l0, l1))
+            add("s", lambda: sc.activation(X("f", p0, p1), t.xw[:].indirect(X("co", l0, l1)), AF.Copy), [("xw", 0, 4096), L("co", l0, l1)], [L("f", p0, p1)], cg(CS))
+            gio = [L("f", p0, p1), L("po", l0, l1)], [L("gq", p0, p1)], cg(CS)
+            if (st, u) in GS:
+                add("s", lambda: sc.activation(X("gq", p0, p1), win(), AF.Copy), *gio)
             else:
-                add("v", lambda: v.tensor_copy(t.cw[:, cs:ce].indirect(x("ls")[:, 0:4]), x("ci")[:]), [L("ci"), L("ls", 0, 4)], [("cw", cs, ce)], (0.05 + 3.8 * 64 * CYC) * FAC)
+                add("v", lambda: v.tensor_copy(X("gq", p0, p1), win()), *gio)
+            add("t", [lambda: te.matmul(t[DB][:, 256:256 + CS], t.idb[:], X("f", p0, p1), True, False), lambda: te.matmul(t[DB][:, 256:256 + CS], t.nid[:], X("gq", p0, p1), False, True)],
+                [IDB, NID, L("f", p0, p1), L("gq", p0, p1)], [ALL(DB)], ct(2 * CS))
+            add("s", lambda: sc.activation(X("a", p0, p1), t[DB][:, 256:256 + CS], AF.Abs), [ALL(DB)], [L("a", p0, p1)], cv(CS))
+            add("v", lambda: v.tensor_tensor(X("m", p0, p1), X("a", p0, p1), t[lb][:, c0:c0 + CS], ALU.is_le), [L("a", p0, p1), ALL(lb)], [L("m", p0, p1)], cv(CS))
+
+        def key_and_hop():
+            add("t", lambda: te.matmul(t[QB][0:LB, 232:240], X("pa"), t.bo[:, 0::16], True, True), [L("pa"), BO], [ALL(QB)], ct(64))
+            add("t", lambda: te.matmul(t[LX[1]][0:LB, 0:128], X("pa"), t.bo[:], True, True), [L("pa"), BO], [ALL(LX[1])], ct(128))
+            add("s", lambda: sc.activation(X("f8", 0, 16, LB), t[QB][0:LB, 224:240], AF.Relu, bias=t.bias[0:LB, 0:1], accum_out=X("mm", 0, 1, LB)),
+                [ALL(QB), ("bias", 0, 1)], [L("f8"), L("mm")], cv(64) + 0.02)
+            add("v", lambda: v.tensor_tensor(X("mk", 0, 128, LB), t.ml[0:LB, :], t[LX[1]][0:LB, 0:128], ALU.mult), [ALL(LX[1]), ML], [L("mk")], cv(128))
+            add("v", lambda: v.tensor_copy(X("mn", 0, 1, LB), X("mm", 0, 1, LB)), [L("mm")], [L("mn")], cv(1))
+            add("v", lambda: v.tensor_scalar(X("od", 0, 1, LB), X("mn", 0, 1, LB), 1, None, ALU.bitwise_and), [L("mn")], [L("od")], cv(1))
+            add("v", lambda: v.tensor_scalar(t.mout[0:LB, q0 + LB:q0 + LB + 1], X("od", 0, 1, LB), t.minb[0:LB, o + LB:o + LB + 1], 1.0, ALU.add, ALU.add),
+                [L("od"), ("minb", o + LB, o + LB + 8)], [("mout", q0 + LB, q0 + LB + 4)], cv(1))
+            add("v", lambda: v.tensor_scalar(X("rb", 0, LB, LB), t.e4s[0:LB, :], t.mout[0:LB, q0 + LB:q0 + LB + 1], None, ALU.mult),
+                [("mout", q0 + LB, q0 + LB + 4), ("e4s", 0, LB)], [L("rb")], cv(LB))
+            add("v", lambda: v.tensor_tensor(X("ns"), MI.indirect(t.cl[:, 0:H]), U, ALU.not_equal), [MIR, ("cl", 0, H), UR], [L("ns")], cg(LB))
+            add("s", lambda: sc.activation(X("se"), X("ns"), AF.Copy, bias=1.0, scale=-1.0), [L("ns")], [L("se")], cv(LB))
+            add("v", lambda: v.tensor_tensor(X("ua"), X("ns"), U, ALU.mult), [L("ns"), UR], [L("ua")], cv(2 * LB))
+            N0, N1, S0, S1 = 384, 384 + H, slice(256, 256 + LB), slice(320, 320 + LB)
+            if s < N - 1:
+                for j in range(H):
+                    add("v", lambda j=j: v.tensor_reduce(X("mo", j, j + 1), X("ua", j, None, 128, H), AxisListType.X, ALU.max), [L("ua")], [L("mo", j, j + 1)], cv(16))
+                add("v", lambda: v.tensor_scalar(X("lk", 0, H), X("li", 0, H), 65536.0, None, ALU.add), [L("li")], [L("lk")], cv(4))
+                add("t", [lambda: te.matmul(t[LX[0]][:, N0:N1], t.idf[:], X("lk", 0, H), True, False),
+                          lambda: te.matmul(t[LX[0]][:, N0:N1], X("mk", 0, 128, LB), t.e4n[0:LB, 0:H], False, False)],
+                    [IDF, L("lk"), L("mk"), ("e4n", 0, LB)], [ALL(LX[0])], ct(320))
+                add("t", lambda: te.matmul(t[LX[0]][:, N0:N1], t.ml[0:LB, :], X("rb", 0, H, LB), False, True), [ML, L("rb")], [ALL(LX[0])], ct(64))
+                add("v", lambda: v.tensor_tensor(t.mxo[:, k0:k0 + H], X("mo", 0, H), t[LX[0]][:, N0:N1], ALU.max), [ALL(LX[0]), L("mo")], [("mxo", k0, k0 + H)], cv(8))
+                k1, ks = k0 + 8 * NB, "k%d_%d" % (s + 1, b)
+                snd = add("g", lambda: g.remote_dma(t.mia[:, k1:k1 + H], t.mxo[:, k0:k0 + H], t.sem[ks], t.sem.lsem, npid, nrid, nmask),
+                          [("mxo", k0, k0 + H)], (), 1.0, "lsem", -nne)
+                add("r", [], (), [("mia", k1, k1 + H)], HOP, ks, nne, (snd,))
+            add("t", [lambda: te.matmul(t[LX[0]][:, S0], t.idf[:], t.ck[:], True, False),
+                      lambda: te.matmul(t[LX[0]][:, S0], X("mk", 0, 128, LB), t.e4n[0:LB, :], False, False)],
+                [IDF, CK, L("mk"), ("e4n", 0, LB)], [ALL(LX[0])], ct(320))
+            add("t", lambda: te.matmul(t[LX[0]][:, S0], t.ml[0:LB, :], X("rb", 0, LB, LB), False, True), [ML, L("rb")], [ALL(LX[0])], ct(64))
+            add("v", lambda: v.tensor_tensor(t[LX[0]][:, S1], X("se"), t[LX[0]][:, S0], ALU.mult), [L("se"), ALL(LX[0])], [ALL(LX[0])], cv(LB))
+            add("v", lambda: v.tensor_tensor(t.mout[:, q0:q0 + LB], t[LX[0]][:, S1], X("ua"), ALU.add), [ALL(LX[0]), L("ua")], [("mout", q0, q0 + LB)], cv(LB))
+            add("t", [lambda: te.matmul(t[LX[1]][0:LB, 128:136], t.idf[0:LB, 0:LB], t.minb[0:LB, o + LB + 8:o + MW], True, False)] +
+                [lambda k=k: te.matmul(t[LX[1]][0:LB, 128:136], t.idb[0:LB, 0:LB], X("f8", 8 * k, 8 * k + 8, LB), False, k == 1) for k in range(2)],
+                [IDF, IDB, ("minb", o + LB + 8, o + MW), L("f8")], [ALL(LX[1])], ct(384))
+            add("s", lambda: sc.activation(t.mout[0:LB, q0 + LB + 8:q0 + MW], t[LX[1]][0:LB, 128:136], AF.Copy), [ALL(LX[1])], [("mout", q0 + LB + 8, q0 + MW)], cv(64))
+            hs, no = "h%d_%d" % (s + 1, b), mi(s + 1, b)
+            snd = add("g", lambda: g.remote_dma(t.minb[:, no:no + MW], t.mout[:, q0:q0 + MW], t.sem[hs], t.sem.lsem, npid, nrid, nmask),
+                      [("mout", q0, q0 + MW)], (), 1.0, "lsem", -nne)
+            add("r", [], (), [("minb", no, no + MW)], HOP + 0.5, hs, nne, (snd,))
+
+        def step(st):
+            BK = (QB, RB)[st]
+            if st == 1:
+                add("v", lambda: v.tensor_copy(X("cf"), X("ci")), [L("ci")], [L("cf")], cv(LB))
+            for u in range(NS):
+                piece(st, u)
+            add("s", lambda: sc.activation(X("a5"), X("cf"), AF.Copy, bias=float(1 - 17 * KB), scale=5.0), [L("cf")], [L("a5")], cv(LB))
+            add("s", lambda: sc.activation(X("ax"), X("cf"), AF.Copy, bias=float(1 - 17 * KB + THR), scale=5.0), [L("cf")], [L("ax")], cv(LB))
+            add("t", lambda: te.matmul(t[RB][:, 0:LB], t.idf[:], X("a5"), True, False), [IDF, L("a5")], [ALL(RB)], ct(256))
+            add("t", [lambda k=k: te.matmul(t[RB][:, 0:LB], t.es[:, 128 * k:128 * k + 128], X("a", k, None, 128, 16), False, False) for k in range(16)],
+                [("es", 0, 2048), L("a")], [ALL(RB)], ct(1024))
+            add("t", [lambda k=k: te.matmul(t[RB][:, 0:LB], t.ew[:, 128 * k:128 * k + 128], X("m", k, None, 128, 16), False, k == 15) for k in range(16)],
+                [("ew", 0, 2048), L("m")], [ALL(RB)], ct(1024))
+
+            def qc():
+                add("t", lambda: te.matmul(t[BK][:, 128:128 + LB], t.idf[:], X("cf"), True, False), [IDF, L("cf")], [ALL(BK)], ct(256))
+
+            def qp():
+                add("t", lambda: te.matmul(t[BK][:, 128:128 + LB], t.bq[:], X("pa"), False, True), [("bq", 0, 128), L("pa")], [ALL(BK)], ct(64))
+
+            def bm():
+                add("v", lambda: v.tensor_tensor(X("bm"), X("ax"), t[RB][:, 0:LB], ALU.min), [L("ax"), ALL(RB)], [L("bm")], cv(LB))
+            if st == 0:
+                qc()
+            add("v", lambda: v.tensor_scalar(X("pa"), t[RB][:, 0:LB], float(THR - 17 * KB), None, ALU.is_ge), [ALL(RB)], [L("pa")], cv(LB))
+            if st == 0:
+                qp()
+                bm()
+            else:
+                key_and_hop()
+                bm()
+                qc()
+                qp()
+            add("v", lambda: v.tensor_tensor(X("yi"), X("bm"), t[BK][:, 128:128 + LB], ALU.min), [L("bm"), ALL(BK)], [L("yi")], cv(LB))
+            add("v", lambda: v.tensor_scalar(X("ci"), X("yi"), 4095, None, ALU.bitwise_and), [L("yi")], [L("ci")], cv(LB))
+            if st == 0:
+                add("v", lambda: v.tensor_copy(X("co"), X("ci")), [L("ci")], [L("co")], cv(LB))
+                add("t", lambda: te.matmul(t[QB][0:LB, 224:232], X("pa"), t.bo[:, 0::16], True, True), [L("pa"), BO], [ALL(QB)], ct(64))
+            else:
+                add("v", lambda: v.tensor_copy(t.cw[:, cs:ce].indirect(X("ls", 0, H)), X("ci")), [L("ci"), L("ls")], [("cw", cs, ce)], (0.05 + 3.8 * LB * CYC) * FAC)
+        step(0)
+        step(1)
         if s == N - 1:
             add("y", lambda: g.sync.dma_start(t.yg[:, cs:ce], t.cw[:, cs:ce]), [("cw", cs, ce)], (), 0.06, nm("oyg", b), 16, (), 4.0)
 
@@ -352,22 +381,23 @@ def rank_program(g, core, T, topo):
             slice_block(s, b)
     cur[0] = 0.0
 
-    for b in range(NB):
+    def home(b):
+        L, X, LX, RB, QB = tiles(b)
         o = mi(N, b)
-        L0, L1 = nm("pb", 2 * b), nm("pb", 2 * b + 1)
-        x = lambda n, b=b: t[nm(n, b)]
-        add("s", lambda o=o, x=x: sc.activation(x("rb")[0:64, :], t.e4[0:64, :], AF.Identity, scale=t.minb[0:64, o + 64:o + 65]), [("e4", 0, 64), ("minb", o + 64, o + 72)], [(nm("rb", b), 0, 64)], cv(64))
-        add("t", [lambda o=o, L0=L0: te.matmul(t[L0][0:64, 0:128], t.minb[:, o:o + 64], t.idp[:], True, False),
-                  lambda L0=L0: te.matmul(t[L0][0:64, 0:128], t.ck[:], t.idn[:], False, False),
-                  lambda L0=L0, x=x: te.matmul(t[L0][0:64, 0:128], x("rb")[0:64, :], t.ml[0:64, :], False, True)],
-            [("minb", o, o + 64), ("idn", 0, 128), CK, ("idp", 0, 128), (nm("rb", b), 0, 64), ("ml", 0, 128)], [(L0, 0, 512)], ct(1152))
-        add("v", lambda L0=L0, x=x: v.tensor_copy(x("vo")[0:64, :], t[L0][0:64, 0:128]), [(L0, 0, 512)], [(nm("vo", b), 0, 128)], cv(128))
+        L0, L1 = t[LX[0]][0:LB, 256:384], t[LX[1]][0:8, 0:LB]
+        add("s", lambda: sc.activation(X("rb", 0, LB, LB), t.e4[0:LB, :], AF.Identity, scale=t.minb[0:LB, o + LB:o + LB + 1]), [E4, ("minb", o + LB, o + LB + 8)], [L("rb")], cv(LB))
+        add("t", [lambda: te.matmul(L0, t.minb[:, o:o + LB], t.idp[:], True, False), lambda: te.matmul(L0, t.ck[:], t.idn[:], False, False),
+                  lambda: te.matmul(L0, X("rb", 0, LB, LB), t.ml[0:LB, :], False, True)],
+            [("minb", o, o + LB), ("idn", 0, 128), CK, ("idp", 0, 128), L("rb"), ML], [ALL(LX[0])], ct(1152))
+        add("v", lambda: v.tensor_copy(X("vo", 0, 128, LB), L0), [ALL(LX[0])], [L("vo")], cv(128))
         for (q, k0) in (("y", 0), ("s", 4)):
-            add(q, [lambda b=b, k=k, q=q, x=x: eng[q].dma_start(t.yv[16 * k:16 * k + 16, 64 * b:64 * b + 64], x("vo")[0:64, 16 * k:16 * k + 16]) for k in range(k0, k0 + 4)],
-                [(nm("vo", b), 0, 128)], (), 0.24, nm("oyv", b), 64 if q == "y" else 128, (), 2.0)
-        add("t", lambda o=o, L1=L1: te.matmul(t[L1][0:8, 0:64], t.minb[0:64, o + 72:o + 80], t.idf[0:64, 0:64], True, True), [("minb", o + 72, o + 80), IDF], [(L1, 0, 512)], ct(256))
-        add("s", lambda L1=L1, x=x: sc.activation(x("yo")[0:8, :], t[L1][0:8, 0:64], AF.Copy), [(L1, 0, 512)], [(nm("yo", b), 0, 64)], cv(64))
-        add("y", lambda b=b, x=x: g.sync.dma_start(t.ym[:, 64 * b:64 * b + 64], x("yo")[0:8, :]), [(nm("yo", b), 0, 64)], (), 0.06, nm("oym", b), 16, (), 2.0)
+            add(q, [lambda k=k, q=q: eng[q].dma_start(t.yv[16 * k:16 * k + 16, LB * b:LB * b + LB], X("vo", 16 * k, 16 * k + 16, LB)) for k in range(k0, k0 + 4)],
+                [L("vo")], (), 0.24, nm("oyv", b), 64 if q == "y" else 128, (), 2.0)
+        add("t", lambda: te.matmul(L1, t.minb[0:LB, o + LB + 8:o + MW], t.idf[0:LB, 0:LB], True, True), [("minb", o + LB + 8, o + MW), IDF], [ALL(LX[1])], ct(256))
+        add("s", lambda: sc.activation(X("yo", 0, LB, 8), L1, AF.Copy), [ALL(LX[1])], [L("yo")], cv(64))
+        add("y", lambda: g.sync.dma_start(t.ym[:, LB * b:LB * b + LB], X("yo", 0, LB, 8)), [L("yo")], (), 0.06, nm("oym", b), 16, (), 2.0)
+    for b in range(NB):
+        home(b)
 
     order = schedule(nodes)
     pos = {i: k for k, i in enumerate(order)}

from concourse.bass import DstId, RemoteDMATransfer
from concourse.mybir import AluOpType as ALU, AxisListType, ActivationFunctionType as AF

N, NB = 8, 2
LB = 128 // NB
H = LB // 16
LS = 16
NS = LB // LS
CB, CS = 16 * LB, 16 * LS
MW = LB + 16
GS = ((1, NS - 1),)
BON, LOOK, HOLD = 3.0, 0.1, 0.4
KB = 1 << 19
W15 = 1 << 15
THR = 10 * W15

SCRATCH = {
    "xw": ("sbuf", [128, 4096], "bfloat16"), "pw": ("sbuf", [128, 2048], "bfloat16"),
    "pgi": ("sbuf", [128, 2048], "int32"), "cw": ("sbuf", [128, 2048], "float32"),
    "vt": ("sbuf", [128, 128], "int32"), "vtb": ("sbuf", [128, 128], "bfloat16"),
    "limo": ("sbuf", [128, 128], "bfloat16"), "limt": ("sbuf", [128, 128 * N], "bfloat16"),
    "minb": ("sbuf", [128, MW * NB * (N + 1)], "float32"), "mout": ("sbuf", [128, MW * NB * N], "float32"),
    "mia": ("sbuf", [128, 8 * NB * N], "int32"), "mxo": ("sbuf", [128, 8 * NB * N], "int32"),
    "onef": ("sbuf", [128, 128], "float32"), "oneb": ("sbuf", [128, 128], "bfloat16"), "posb": ("sbuf", [128, 128], "bfloat16"),
    "bias": ("sbuf", [128, 1], "float32"),
    "idf": ("sbuf", [128, 128], "float32"), "idb": ("sbuf", [128, 128], "bfloat16"), "nid": ("sbuf", [128, 128], "bfloat16"),
    "idp": ("sbuf", [128, 128], "float32"), "idn": ("sbuf", [128, 128], "float32"),
    "bo0": ("sbuf", [128, 128], "bfloat16"), "bo": ("sbuf", [128, 128], "bfloat16"),
    "bq1": ("sbuf", [128, 128], "float32"), "bq2": ("sbuf", [128, 128], "float32"), "bq": ("sbuf", [128, 128], "bfloat16"),
    "pmt": ("sbuf", [128, 128], "bfloat16"), "es": ("sbuf", [128, 2048], "bfloat16"), "ew": ("sbuf", [128, 2048], "bfloat16"),
    "ex": ("sbuf", [128, 2048], "bfloat16"),
    "ix": ("sbuf", [128, 128], "int32"), "ix2": ("sbuf", [128, 128], "int32"), "ml": ("sbuf", [128, 128], "bfloat16"),
    "ka": ("sbuf", [128, LB], "int32"), "ka2": ("sbuf", [128, LB], "int32"), "kb": ("sbuf", [128, LB], "int32"), "ck": ("sbuf", [128, LB], "float32"),
    "r16": ("sbuf", [128, LB], "bfloat16"), "cli": ("sbuf", [128, H], "int32"), "cli2": ("sbuf", [128, H], "int32"), "cl": ("sbuf", [128, H], "uint16"),
    "e4a": ("sbuf", [128, LB], "bfloat16"), "e4": ("sbuf", [128, LB], "bfloat16"), "e4s": ("sbuf", [128, LB], "bfloat16"), "e4n": ("sbuf", [128, LB], "bfloat16"),
}
TILE = {"f": (CB, "bfloat16"), "gq": (CB, "bfloat16"), "a": (CB, "bfloat16"), "m": (CB, "bfloat16"), "li": (4, "int32"), "ls": (4, "uint16"),
        "cf": (LB, "float32"), "co": (LB, "uint16"), "lk": (4, "float32"), "mo": (4, "float32"), "pg_": (LB, "bfloat16"), "po": (LB, "uint16"),
        "a5": (LB, "float32"), "ax": (LB, "float32"), "pa": (LB, "bfloat16"), "bm": (LB, "float32"), "yi": (LB, "int32"), "ci": (LB, "int32"),
        "f8": (16, "bfloat16"), "mm": (4, "float32"), "mn": (4, "int32"), "od": (4, "int32"), "rb": (LB, "bfloat16"), "mk": (128, "bfloat16"),
        "ns": (LB, "float32"), "se": (LB, "float32"), "ua": (LB, "float32"), "vo": (128, "float32"), "yo": (LB, "float32")}
for _n in TILE:
    SCRATCH[_n] = ("sbuf", [128, NB * TILE[_n][0]], TILE[_n][1])
for _b in range(8):
    SCRATCH["pb%d" % _b] = ("psum", [128, 512], "float32")

SEMAPHORES = ["qv", "qs", "qt", "qg", "lsem", "limr", "dlim", "dvv", "dxt"]
SEMAPHORES += ["%s%d" % (n, b) for n in ("dpg", "dpre", "oyg", "oyv", "oym") for b in range(NB)]
SEMAPHORES += ["h%d_%d" % (s, b) for s in range(1, N + 1) for b in range(NB)] + ["k%d_%d" % (s, b) for s in range(1, N) for b in range(NB)]

CYC, FAC, WAKE, XG, PEC, HOP = 0.00083, 1.0, 0.2, 1.56, 0.0004, 4.0


def cv(n):
    return max(64, n) * CYC * FAC


def cg(n):
    return (0.055 + XG * n * CYC) * FAC


def ct(n):
    return n * PEC


def schedule(nodes):
    n = len(nodes)
    succ = [[] for _ in range(n)]
    for i, d in enumerate(nodes):
        for j in d["dep"]:
            succ[j].append(i)
    pri = [0.0] * n
    for i in range(n - 1, -1, -1):
        d = nodes[i]
        pri[i] = d["c"] + d["lat"] + WAKE + max([pri[k] for k in succ[i]] + [0.0])
    for i in range(n):
        pri[i] -= nodes[i]["bl"]
    left = [len(d["dep"]) for d in nodes]
    ready = [0.0] * n
    free = {"v": 0.0, "s": 0.0, "t": 0.0, "g": 0.0, "y": 0.0}
    pool = {q: [] for q in list(free) + ["r"]}
    for i in range(n):
        if left[i] == 0:
            pool[nodes[i]["q"]].append(i)
    order = []
    while len(order) < n:
        best = None
        for q in pool:
            if not pool[q]:
                continue
            f = free.get(q, 0.0)
            t0 = min(max(f, ready[i]) for i in pool[q])
            i = max((i for i in pool[q] if max(f, ready[i]) <= t0 + LOOK), key=lambda i: pri[i])
            e0 = max(f, ready[i]) + HOLD * nodes[i]["c"]
            i = max((j for j in pool[q] if ready[j] <= e0), key=lambda j: pri[j])
            st = max(f, ready[i])
            if best is None or st < best[0]:
                best = (st, q, i)
        st, q, i = best
        pool[q].remove(i)
        en = st + nodes[i]["c"]
        if q != "r":
            free[q] = en
        order.append(i)
        for k in succ[i]:
            w = 0.0 if (nodes[k]["q"] == q and not nodes[k]["dep"][i]) else WAKE
            ready[k] = max(ready[k], en + nodes[i]["lat"] + w)
            left[k] -= 1
            if left[k] == 0:
                pool[nodes[k]["q"]].append(k)
    return order


def rank_program(g, core, T, topo):
    rank = T.rank_of(core)
    if rank is None:
        return
    eng = {"v": g.vector, "s": g.scalar, "t": g.tensor, "g": g, "y": g.sync}
    csem = {"v": "qv", "s": "qs", "t": "qt", "g": "qg"}
    nodes, last, cur = [], {}, [0.0]
    STREAM = ("ls", "co", "po", "cw", "f")

    def add(q, fns, R=(), W=(), c=0.08, sem=None, val=None, after=(), lat=0.0):
        i = len(nodes)
        dep = {}
        for (acc, wr) in ((R, False), (W, True)):
            for (buf, a, b) in acc:
                bank = buf[:2] == "pb"
                rec = last.setdefault(buf, [])
                for (j, ja, jb, jw) in rec:
                    if j == i or (not bank and (ja >= b or jb <= a)):
                        continue
                    same = nodes[j]["q"] == q
                    if not (wr or jw) and (same or not bank):
                        continue
                    need = not (same and (q == "t" or not (jw or buf in STREAM)))
                    dep[j] = dep.get(j, False) or need
                if wr:
                    if bank and q == "t":
                        rec[:] = [r for r in rec if r[0] == i]
                    elif not bank:
                        rec[:] = [r for r in rec if r[0] == i or not (r[1] >= a and r[2] <= b)]
                rec.append((i, a, b, wr))
        for j in after:
            dep[j] = dep.get(j, False)
        nodes.append({"q": q, "f": fns if isinstance(fns, list) else [fns], "dep": dep, "c": c, "sem": sem, "val": val, "lat": lat, "bl": cur[0]})
        return i

    t = T
    nm = lambda n, b: "%s%d" % (n, b)
    v, sc, te = g.vector, g.scalar, g.tensor
    IDF, CK, IDB, NID, BO, ML, E4 = ("idf", 0, 128), ("ck", 0, LB), ("idb", 0, 128), ("nid", 0, 128), ("bo", 0, 128), ("ml", 0, 128), ("e4", 0, LB)

    def load(fns, W, sem, cost, q="y"):
        add(q, fns, (), W, 0.06 * len(fns), sem, 16 * len(fns), (), cost)
    load([lambda k=k: g.scalar.dma_start(t.vt[:, 16 * k:16 * k + 16], t.vv[16 * k:16 * k + 16, :]) for k in range(8)], [("vt", 0, 128)], "dvv", 3.0, "s")
    load([lambda: g.sync.dma_start(t.limo[:], t.lim[:])], [("limo", 0, 128)], "dlim", 2.5)
    for b in range(NB):
        load([lambda b=b: g.sync.dma_start(t.pgi[:, CB * b:CB * b + CB], t.pg[:, CB * b:CB * b + CB])], [("pgi", CB * b, CB * b + CB)], nm("dpg", b), 4.5 + 5.5 * b)
        if b == 0:
            load([lambda: g.sync.dma_start(t.xw[:], t.xt[:])], [("xw", 0, 4096)], "dxt", 7.0)
        load([lambda b=b: g.sync.dma_start(t.pw[:, CB * b:CB * b + CB], t.pre[:, CB * b:CB * b + CB])], [("pw", CB * b, CB * b + CB)], nm("dpre", b), 7.5 + 4.0 * b)

    def vmem(buf, a, b, val):
        add("v", lambda: v.memset(t[buf][:, a:b], val), (), [(buf, a, b)], cv((b - a) * (0.5 if SCRATCH[buf][2] == "bfloat16" else 1)))

    def vts(out, in0, n, fn, half=False):
        add("v", fn, [(in0, 0, n)], [(out, 0, n)], cv(n * (0.5 if half else 1)))

    def gen(out, n, fn, in_=None):
        add("g", fn, [(in_, 0, n)] if in_ else (), [(out, 0, n)], (0.17 + 2 * n * CYC) * FAC)
    vmem("onef", 0, 128, 1.0)
    vmem("oneb", 0, 128, 1.0)
    vmem("posb", 0, 128, 1024.0)
    vmem("bias", 0, 1, -15.0)
    gen("idf", 128, lambda: g.affine_select(t.idf[:], t.onef[:], [[-1, 128]], ALU.is_equal, 0.0, 0, 1), "onef")
    gen("pmt", 128, lambda: g.affine_select(t.pmt[:], t.posb[:], [[-H, NB], [-8, 16], [-1, H]], ALU.is_equal, 0.0, 0, 1), "posb")
    gen("ka", LB, lambda: g.iota(t.ka[:], [[0, LB]], 0, 16))
    gen("kb", LB, lambda: g.iota(t.kb[:], [[-1, 16], [-256, H]], 65536 + 1023, 0))
    gen("cli", H, lambda: g.iota(t.cli[:], [[0, H]], 0, 1))
    gen("r16", LB, lambda: g.iota(t.r16[:], [[0, NS], [16, LS]], 0, 0, allow_small_or_imprecise_dtypes=True))
    gen("bo0", 128, lambda: g.affine_select(t.bo0[:], t.oneb[:], [[-16, 8], [0, 16]], ALU.is_ge, 0.0, 0, 1), "oneb")
    gen("bo", 128, lambda: g.affine_select(t.bo[:], t.bo0[:], [[16, 8], [0, 16]], ALU.is_ge, 0.0, 15, -1), "bo0")
    gen("es", 2048, lambda: g.iota(t.es[:], [[0, 2048]], 0, 0, allow_small_or_imprecise_dtypes=True))
    gen("ix", 128, lambda: g.iota(t.ix[:], [[-1, 128]], 128, 1))
    gen("e4a", LB, lambda: g.affine_select(t.e4a[:], t.oneb[:, 0:LB], [[0, 16], [-16, H]], ALU.is_ge, 0.0, 0, 1), "oneb")
    gen("e4", LB, lambda: g.affine_select(t.e4[:], t.e4a[:], [[0, 16], [16, H]], ALU.is_ge, 0.0, 15, -1), "e4a")
    gen("mout", MW * NB * N, lambda: g.iota(t.mout[:], [[0, MW * NB * N]], 0, 0, allow_small_or_imprecise_dtypes=True))
    vts("idb", "idf", 128, lambda: v.tensor_copy(t.idb[:], t.idf[:]))
    add("v", lambda: v.tensor_copy(t.vtb[:], t.vt[:]), [("vt", 0, 128)], [("vtb", 0, 128)], cv(128))
    vts("ka2", "ka", LB, lambda: v.tensor_scalar(t.ka2[:], t.ka[:], 255, None, ALU.bitwise_and))
    add("v", lambda: v.tensor_tensor(t.ck[:], t.kb[:], t.ka2[:], ALU.subtract), [("ka2", 0, LB), ("kb", 0, LB)], [CK], cv(2 * LB))
    vts("cli2", "cli", H, lambda: v.tensor_scalar(t.cli2[:], t.cli[:], H - 1, None, ALU.bitwise_and))
    vts("cl", "cli2", H, lambda: v.tensor_copy(t.cl[:], t.cli2[:]))
    for b in range(NB):
        add("v", lambda b=b: v.tensor_copy(t.cw[:, CB * b:CB * b + CB], t.pgi[:, CB * b:CB * b + CB]), [("pgi", CB * b, CB * b + CB)], [("cw", CB * b, CB * b + CB)], cv(CB))

    def mi(s, b):
        return MW * (NB * s + b)
    for b in range(NB):
        o = mi(0, b)
        pb = nm("pb", 6 + b)
        add("t", [lambda b=b, pb=pb: te.matmul(t[pb][:, 448:448 + LB], t.vtb[:], t.pmt[:, LB * b:LB * b + LB], True, True)],
            [("vtb", 0, 128), ("pmt", 0, 128)], [(pb, 0, 512)], ct(64))
        add("v", lambda o=o, pb=pb: v.tensor_tensor(t.minb[:, o:o + LB], t.ck[:], t[pb][:, 448:448 + LB], ALU.add), [(pb, 0, 512), CK], [("minb", o, o + LB)], cv(LB))
        vmem("minb", o + LB, o + MW, 0.0)
        for j in range(H):
            add("v", lambda j=j, b=b, o=o: v.tensor_reduce(t.mia[:, 8 * b + j:8 * b + j + 1], t.minb[:, o + j:o + LB:H], AxisListType.X, ALU.max),
                [("minb", o, o + LB)], [("mia", 8 * b + j, 8 * b + j + 1)], cv(16))
    add("t", lambda: te.matmul(t.pb0[:, 0:128], t.limo[:], t.idb[:], True, True), [("limo", 0, 128), IDB], [("pb0", 0, 512)], ct(128))
    add("s", lambda: sc.activation(t.limt[:, 0:128], t.pb0[:, 0:128], AF.Copy), [("pb0", 0, 512)], [("limt", 0, 128)], cv(128))
    nxt = T.cores[(rank + 1) % N]
    nrid, npid, _ = topo.addr(nxt)
    nmask = topo.mask(core, nxt)
    nne = bin(nmask).count("1")
    dst, dsts, mask = [], [], nmask
    for s in range(1, N):
        d = T.cores[(rank + s) % N]
        rid, pid, _ = topo.addr(d)
        mask &= topo.mask(core, d)
        dst.append(DstId(rid=rid, pnc=pid))
        dsts.append(t.limt[:, 128 * s:128 * s + 128])
    ne = bin(mask).count("1")
    limsend = add("g", lambda: g.remote_dma_fused([RemoteDMATransfer(dst_ids=dst, dma_engine_mask=mask, remote_sem=t.sem.limr,
                  srcs=[t.limt[:, 0:128]], dsts=dsts)], local_sem=t.sem.lsem), [("limt", 0, 128)], (), 2.0, "lsem", -ne)
    add("r", [], (), [("limt", 128, 128 * N)], 4.0, "limr", 7 * ne, (limsend,))

    for k in range(16):
        add("s", lambda k=k: sc.activation(t.ex[:, k::16], t.idb[:], AF.Copy), [IDB], [("ex", 0, 2048)], cv(128))
    for k in range(16):
        add("v", lambda k=k: v.tensor_copy(t.es[:, 128 * k + k:128 * k + 128:16], t.bo[:, k::16]), [BO], [("es", 128 * k, 128 * k + 128)], cv(8))
    add("v", lambda: v.tensor_scalar(t.ew[:], t.es[:], float(W15), None, ALU.mult), [("es", 0, 2048)], [("ew", 0, 2048)], cv(1024))
    vts("bq1", "idb", 128, lambda: v.tensor_scalar(t.bq1[:], t.idb[:], float(-32 * KB), None, ALU.mult))
    vts("bq2", "bo", 128, lambda: v.tensor_scalar(t.bq2[:], t.bo[:], float(KB), None, ALU.mult))
    add("v", lambda: v.tensor_tensor(t.bq[:], t.bq1[:], t.bq2[:], ALU.add), [("bq1", 0, 128), ("bq2", 0, 128)], [("bq", 0, 128)], cv(256))
    vts("nid", "idb", 128, lambda: v.tensor_scalar(t.nid[:], t.idb[:], -1.0, None, ALU.mult), True)
    vts("ix2", "ix", 128, lambda: v.tensor_scalar(t.ix2[:], t.ix[:], 15, None, ALU.bitwise_and))
    vts("ml", "ix2", 128, lambda: v.tensor_scalar(t.ml[:], t.ix2[:], 0.0, None, ALU.is_equal))
    vts("e4s", "e4", LB, lambda: v.tensor_scalar(t.e4s[:], t.e4[:], -1024.0, None, ALU.mult), True)
    vts("e4n", "e4", LB, lambda: v.tensor_scalar(t.e4n[:], t.e4[:], 1024.0, None, ALU.mult), True)
    vts("idp", "idf", 128, lambda: v.tensor_scalar(t.idp[:], t.idf[:], 1.0 / 1024, None, ALU.mult))
    vts("idn", "idf", 128, lambda: v.tensor_scalar(t.idn[:], t.idf[:], -1.0 / 1024, None, ALU.mult))

    def tiles(b):
        def L(n, a=0, e=None):
            w = TILE[n][0]
            return (n, w * b + a, w * b + (w if e is None else e))

        def X(n, a=0, e=None, p=128, st=1):
            _, c0, c1 = L(n, a, e)
            return t[n][0:p, c0:c1:st] if st > 1 else t[n][0:p, c0:c1]
        return L, X, [nm("pb", 2 * b), nm("pb", 2 * b + 1)], nm("pb", 4 + b), nm("pb", 6 + b)
    ALL = lambda bank: (bank, 0, 512)

    def slice_block(s, b):
        L, X, LX, RB, QB = tiles(b)
        o, q0 = mi(s, b), MW * (NB * s + b)
        U, UR = t.minb[:, o:o + LB], ("minb", o, o + LB)
        cs, ce = CB * b, CB * b + CB
        k0 = 8 * (NB * s + b)
        MI, MIR = t.mia[:, k0:k0 + H], ("mia", k0, k0 + H)
        add("v", lambda: v.tensor_scalar(X("li", 0, H), MI, 1023, None, ALU.bitwise_and), [MIR], [L("li")], cv(H))
        add("v", lambda: v.tensor_scalar(X("ls", 0, H), X("li", 0, H), -1.0, 1023.0, ALU.mult, ALU.add), [L("li")], [L("ls")], cv(H))
        add("v", lambda: v.tensor_copy(X("co"), t.cw[:, cs:ce].indirect(X("ls", 0, H))), [("cw", cs, ce), L("ls")], [L("co")], cg(LB))
        add("s", lambda: sc.activation(X("cf"), t.cw[:, cs:ce].indirect(X("ls", 0, H)), AF.Copy), [("cw", cs, ce), L("ls")], [L("cf")], cg(LB))
        add("s", lambda: sc.activation(X("pg_"), t.pw[:, cs:ce].indirect(X("ls", 0, H)), AF.Copy), [("pw", cs, ce), L("ls")], [L("pg_")], cg(LB))
        add("t", [lambda: te.matmul(t[QB][:, 64:64 + LB], t.idb[:], X("pg_"), True, False), lambda: te.matmul(t[QB][:, 64:64 + LB], t.idb[:], t.r16[:], False, True)],
            [IDB, L("pg_"), ("r16", 0, LB)], [ALL(QB)], ct(128))
        add("v", lambda: v.tensor_copy(X("po"), t[QB][:, 64:64 + LB]), [ALL(QB)], [L("po")], cv(LB))
        for h in range(2):
            add("t", lambda h=h: te.matmul(t[LX[h]][:], t.limt[:, 128 * s:128 * s + 128], t.ex[:, cs + 512 * h:cs + 512 * h + 512], True, True),
                [("limt", 128 * s, 128 * s + 128), ("ex", 0, 2048)], [ALL(LX[h])], ct(512))

        def piece(st, u):
            p0, p1, l0, l1 = CS * u, CS * u + CS, LS * u, LS * u + LS
            lb, c0, DB = LX[p0 // 512], p0 % 512, (QB, RB)[u % 2]
            win = lambda: X("f", p0, p1).indirect(X("po", l0, l1))
            add("s", lambda: sc.activation(X("f", p0, p1), t.xw[:].indirect(X("co", l0, l1)), AF.Copy), [("xw", 0, 4096), L("co", l0, l1)], [L("f", p0, p1)], cg(CS))
            gio = [L("f", p0, p1), L("po", l0, l1)], [L("gq", p0, p1)], cg(CS)
            if (st, u) in GS:
                add("s", lambda: sc.activation(X("gq", p0, p1), win(), AF.Copy), *gio)
            else:
                add("v", lambda: v.tensor_copy(X("gq", p0, p1), win()), *gio)
            add("t", [lambda: te.matmul(t[DB][:, 256:256 + CS], t.idb[:], X("f", p0, p1), True, False), lambda: te.matmul(t[DB][:, 256:256 + CS], t.nid[:], X("gq", p0, p1), False, True)],
                [IDB, NID, L("f", p0, p1), L("gq", p0, p1)], [ALL(DB)], ct(2 * CS))
            add("s", lambda: sc.activation(X("a", p0, p1), t[DB][:, 256:256 + CS], AF.Abs), [ALL(DB)], [L("a", p0, p1)], cv(CS))
            add("v", lambda: v.tensor_tensor(X("m", p0, p1), X("a", p0, p1), t[lb][:, c0:c0 + CS], ALU.is_le), [L("a", p0, p1), ALL(lb)], [L("m", p0, p1)], cv(CS))

        def key_and_hop():
            add("t", lambda: te.matmul(t[QB][0:LB, 232:240], X("pa"), t.bo[:, 0::16], True, True), [L("pa"), BO], [ALL(QB)], ct(64))
            add("t", lambda: te.matmul(t[LX[1]][0:LB, 0:128], X("pa"), t.bo[:], True, True), [L("pa"), BO], [ALL(LX[1])], ct(128))
            add("s", lambda: sc.activation(X("f8", 0, 16, LB), t[QB][0:LB, 224:240], AF.Relu, bias=t.bias[0:LB, 0:1], accum_out=X("mm", 0, 1, LB)),
                [ALL(QB), ("bias", 0, 1)], [L("f8"), L("mm")], cv(64) + 0.02)
            add("v", lambda: v.tensor_tensor(X("mk", 0, 128, LB), t.ml[0:LB, :], t[LX[1]][0:LB, 0:128], ALU.mult), [ALL(LX[1]), ML], [L("mk")], cv(128))
            add("v", lambda: v.tensor_copy(X("mn", 0, 1, LB), X("mm", 0, 1, LB)), [L("mm")], [L("mn")], cv(1))
            add("v", lambda: v.tensor_scalar(X("od", 0, 1, LB), X("mn", 0, 1, LB), 1, None, ALU.bitwise_and), [L("mn")], [L("od")], cv(1))
            add("v", lambda: v.tensor_scalar(t.mout[0:LB, q0 + LB:q0 + LB + 1], X("od", 0, 1, LB), t.minb[0:LB, o + LB:o + LB + 1], 1.0, ALU.add, ALU.add),
                [L("od"), ("minb", o + LB, o + LB + 8)], [("mout", q0 + LB, q0 + LB + 4)], cv(1))
            add("v", lambda: v.tensor_scalar(X("rb", 0, LB, LB), t.e4s[0:LB, :], t.mout[0:LB, q0 + LB:q0 + LB + 1], None, ALU.mult),
                [("mout", q0 + LB, q0 + LB + 4), ("e4s", 0, LB)], [L("rb")], cv(LB))
            add("v", lambda: v.tensor_tensor(X("ns"), MI.indirect(t.cl[:, 0:H]), U, ALU.not_equal), [MIR, ("cl", 0, H), UR], [L("ns")], cg(LB))
            add("s", lambda: sc.activation(X("se"), X("ns"), AF.Copy, bias=1.0, scale=-1.0), [L("ns")], [L("se")], cv(LB))
            add("v", lambda: v.tensor_tensor(X("ua"), X("ns"), U, ALU.mult), [L("ns"), UR], [L("ua")], cv(2 * LB))
            N0, N1, S0, S1 = 384, 384 + H, slice(256, 256 + LB), slice(320, 320 + LB)
            if s < N - 1:
                for j in range(H):
                    add("v", lambda j=j: v.tensor_reduce(X("mo", j, j + 1), X("ua", j, None, 128, H), AxisListType.X, ALU.max), [L("ua")], [L("mo", j, j + 1)], cv(16))
                add("v", lambda: v.tensor_scalar(X("lk", 0, H), X("li", 0, H), 65536.0, None, ALU.add), [L("li")], [L("lk")], cv(4))
                add("t", [lambda: te.matmul(t[LX[0]][:, N0:N1], t.idf[:], X("lk", 0, H), True, False),
                          lambda: te.matmul(t[LX[0]][:, N0:N1], X("mk", 0, 128, LB), t.e4n[0:LB, 0:H], False, False)],
                    [IDF, L("lk"), L("mk"), ("e4n", 0, LB)], [ALL(LX[0])], ct(320))
                add("t", lambda: te.matmul(t[LX[0]][:, N0:N1], t.ml[0:LB, :], X("rb", 0, H, LB), False, True), [ML, L("rb")], [ALL(LX[0])], ct(64))
                add("v", lambda: v.tensor_tensor(t.mxo[:, k0:k0 + H], X("mo", 0, H), t[LX[0]][:, N0:N1], ALU.max), [ALL(LX[0]), L("mo")], [("mxo", k0, k0 + H)], cv(8))
                k1, ks = k0 + 8 * NB, "k%d_%d" % (s + 1, b)
                snd = add("g", lambda: g.remote_dma(t.mia[:, k1:k1 + H], t.mxo[:, k0:k0 + H], t.sem[ks], t.sem.lsem, npid, nrid, nmask),
                          [("mxo", k0, k0 + H)], (), 1.0, "lsem", -nne)
                add("r", [], (), [("mia", k1, k1 + H)], HOP, ks, nne, (snd,))
            add("t", [lambda: te.matmul(t[LX[0]][:, S0], t.idf[:], t.ck[:], True, False),
                      lambda: te.matmul(t[LX[0]][:, S0], X("mk", 0, 128, LB), t.e4n[0:LB, :], False, False)],
                [IDF, CK, L("mk"), ("e4n", 0, LB)], [ALL(LX[0])], ct(320))
            add("t", lambda: te.matmul(t[LX[0]][:, S0], t.ml[0:LB, :], X("rb", 0, LB, LB), False, True), [ML, L("rb")], [ALL(LX[0])], ct(64))
            add("v", lambda: v.tensor_tensor(t[LX[0]][:, S1], X("se"), t[LX[0]][:, S0], ALU.mult), [L("se"), ALL(LX[0])], [ALL(LX[0])], cv(LB))
            add("v", lambda: v.tensor_tensor(t.mout[:, q0:q0 + LB], t[LX[0]][:, S1], X("ua"), ALU.add), [ALL(LX[0]), L("ua")], [("mout", q0, q0 + LB)], cv(LB))
            add("t", [lambda: te.matmul(t[LX[1]][0:LB, 128:136], t.idf[0:LB, 0:LB], t.minb[0:LB, o + LB + 8:o + MW], True, False)] +
                [lambda k=k: te.matmul(t[LX[1]][0:LB, 128:136], t.idb[0:LB, 0:LB], X("f8", 8 * k, 8 * k + 8, LB), False, k == 1) for k in range(2)],
                [IDF, IDB, ("minb", o + LB + 8, o + MW), L("f8")], [ALL(LX[1])], ct(384))
            add("s", lambda: sc.activation(t.mout[0:LB, q0 + LB + 8:q0 + MW], t[LX[1]][0:LB, 128:136], AF.Copy), [ALL(LX[1])], [("mout", q0 + LB + 8, q0 + MW)], cv(64))
            hs, no = "h%d_%d" % (s + 1, b), mi(s + 1, b)
            snd = add("g", lambda: g.remote_dma(t.minb[:, no:no + MW], t.mout[:, q0:q0 + MW], t.sem[hs], t.sem.lsem, npid, nrid, nmask),
                      [("mout", q0, q0 + MW)], (), 1.0, "lsem", -nne)
            add("r", [], (), [("minb", no, no + MW)], HOP + 0.5, hs, nne, (snd,))

        def step(st):
            BK = (QB, RB)[st]
            if st == 1:
                add("v", lambda: v.tensor_copy(X("cf"), X("ci")), [L("ci")], [L("cf")], cv(LB))
            for u in range(NS):
                piece(st, u)
            add("s", lambda: sc.activation(X("a5"), X("cf"), AF.Copy, bias=float(1 - 17 * KB), scale=5.0), [L("cf")], [L("a5")], cv(LB))
            add("s", lambda: sc.activation(X("ax"), X("cf"), AF.Copy, bias=float(1 - 17 * KB + THR), scale=5.0), [L("cf")], [L("ax")], cv(LB))
            add("t", lambda: te.matmul(t[RB][:, 0:LB], t.idf[:], X("a5"), True, False), [IDF, L("a5")], [ALL(RB)], ct(256))
            add("t", [lambda k=k: te.matmul(t[RB][:, 0:LB], t.es[:, 128 * k:128 * k + 128], X("a", k, None, 128, 16), False, False) for k in range(16)],
                [("es", 0, 2048), L("a")], [ALL(RB)], ct(1024))
            add("t", [lambda k=k: te.matmul(t[RB][:, 0:LB], t.ew[:, 128 * k:128 * k + 128], X("m", k, None, 128, 16), False, k == 15) for k in range(16)],
                [("ew", 0, 2048), L("m")], [ALL(RB)], ct(1024))

            def qc():
                add("t", lambda: te.matmul(t[BK][:, 128:128 + LB], t.idf[:], X("cf"), True, False), [IDF, L("cf")], [ALL(BK)], ct(256))

            def qp():
                add("t", lambda: te.matmul(t[BK][:, 128:128 + LB], t.bq[:], X("pa"), False, True), [("bq", 0, 128), L("pa")], [ALL(BK)], ct(64))

            def bm():
                add("v", lambda: v.tensor_tensor(X("bm"), X("ax"), t[RB][:, 0:LB], ALU.min), [L("ax"), ALL(RB)], [L("bm")], cv(LB))
            if st == 0:
                qc()
            add("v", lambda: v.tensor_scalar(X("pa"), t[RB][:, 0:LB], float(THR - 17 * KB), None, ALU.is_ge), [ALL(RB)], [L("pa")], cv(LB))
            if st == 0:
                qp()
                bm()
            else:
                key_and_hop()
                bm()
                qc()
                qp()
            add("v", lambda: v.tensor_tensor(X("yi"), X("bm"), t[BK][:, 128:128 + LB], ALU.min), [L("bm"), ALL(BK)], [L("yi")], cv(LB))
            add("v", lambda: v.tensor_scalar(X("ci"), X("yi"), 4095, None, ALU.bitwise_and), [L("yi")], [L("ci")], cv(LB))
            if st == 0:
                add("v", lambda: v.tensor_copy(X("co"), X("ci")), [L("ci")], [L("co")], cv(LB))
                add("t", lambda: te.matmul(t[QB][0:LB, 224:232], X("pa"), t.bo[:, 0::16], True, True), [L("pa"), BO], [ALL(QB)], ct(64))
            else:
                add("v", lambda: v.tensor_copy(t.cw[:, cs:ce].indirect(X("ls", 0, H)), X("ci")), [L("ci"), L("ls")], [("cw", cs, ce)], (0.05 + 3.8 * LB * CYC) * FAC)
        step(0)
        step(1)
        if s == N - 1:
            add("y", lambda: g.sync.dma_start(t.yg[:, cs:ce], t.cw[:, cs:ce]), [("cw", cs, ce)], (), 0.06, nm("oyg", b), 16, (), 4.0)

    for s in range(N):
        for b in range(NB):
            cur[0] = BON * b
            slice_block(s, b)
    cur[0] = 0.0

    def home(b):
        L, X, LX, RB, QB = tiles(b)
        o = mi(N, b)
        L0, L1 = t[LX[0]][0:LB, 256:384], t[LX[1]][0:8, 0:LB]
        add("s", lambda: sc.activation(X("rb", 0, LB, LB), t.e4[0:LB, :], AF.Identity, scale=t.minb[0:LB, o + LB:o + LB + 1]), [E4, ("minb", o + LB, o + LB + 8)], [L("rb")], cv(LB))
        add("t", [lambda: te.matmul(L0, t.minb[:, o:o + LB], t.idp[:], True, False), lambda: te.matmul(L0, t.ck[:], t.idn[:], False, False),
                  lambda: te.matmul(L0, X("rb", 0, LB, LB), t.ml[0:LB, :], False, True)],
            [("minb", o, o + LB), ("idn", 0, 128), CK, ("idp", 0, 128), L("rb"), ML], [ALL(LX[0])], ct(1152))
        add("v", lambda: v.tensor_copy(X("vo", 0, 128, LB), L0), [ALL(LX[0])], [L("vo")], cv(128))
        for (q, k0) in (("y", 0), ("s", 4)):
            add(q, [lambda k=k, q=q: eng[q].dma_start(t.yv[16 * k:16 * k + 16, LB * b:LB * b + LB], X("vo", 16 * k, 16 * k + 16, LB)) for k in range(k0, k0 + 4)],
                [L("vo")], (), 0.24, nm("oyv", b), 64 if q == "y" else 128, (), 2.0)
        add("t", lambda: te.matmul(L1, t.minb[0:LB, o + LB + 8:o + MW], t.idf[0:LB, 0:LB], True, True), [("minb", o + LB + 8, o + MW), IDF], [ALL(LX[1])], ct(256))
        add("s", lambda: sc.activation(X("yo", 0, LB, 8), L1, AF.Copy), [ALL(LX[1])], [L("yo")], cv(64))
        add("y", lambda: g.sync.dma_start(t.ym[:, LB * b:LB * b + LB], X("yo", 0, LB, 8)), [L("yo")], (), 0.06, nm("oym", b), 16, (), 2.0)
    for b in range(NB):
        home(b)

    order = schedule(nodes)
    pos = {i: k for k, i in enumerate(order)}
    cnt, known, tok, total = {}, {q: {} for q in eng}, {}, {}
    for i in order:
        d = nodes[i]
        q = d["q"]
        if q == "r":
            tok[i] = (d["sem"], d["val"], {})
            total[d["sem"]] = d["val"]
            continue
        kn = known[q]
        for j in sorted(d["dep"], key=lambda j: -pos[j]):
            if not d["dep"][j]:
                continue
            sem, val, jk = tok[j]
            if kn.get(sem, 0) >= val:
                continue
            eng[q].wait_ge(t.sem[sem], val)
            for (a, w) in list(jk.items()) + [(sem, val)]:
                kn[a] = max(kn.get(a, 0), w)
        ins = None
        for f in d["f"]:
            ins = f()
            if d["sem"] and d["val"] > 0:
                ins.then_inc(t.sem[d["sem"]], 16)
        if d["sem"] is None:
            sem = csem[q]
            cnt[sem] = cnt.get(sem, 0) + 1
            ins.then_inc(t.sem[sem], 1)
            tok[i] = (sem, cnt[sem], dict(kn))
            total[sem] = cnt[sem]
        elif d["val"] > 0:
            tok[i] = (d["sem"], d["val"], dict(kn))
            total[d["sem"]] = max(d["val"], total.get(d["sem"], 0))
        else:
            total[d["sem"]] = total.get(d["sem"], 0) - d["val"]
    for sem in total:
        if known["g"].get(sem, 0) < total[sem]:
            g.wait_ge(t.sem[sem], total[sem])
